import numpy as np, ml_dtypes
CORES = [10,34,74,98]
N = 4
BF = ml_dtypes.bfloat16
W, C, H, CAP, RO = 4096, 1024, 1024, 64, 4
L = C >> 2
S16 = np.arange(16)
def owner(m):
    mb = np.zeros((8, W + 1), np.int32); mb[np.arange(8)[:, None, None], m] = np.arange(C)[None, :, None]
    return mb[:, :W]
def tight(m):
    return np.take_along_axis(m, np.argsort(m >= W, axis=-1, kind="stable"), -1)
def pick(a, j):
    return np.take_along_axis(a, j[:, :, None], 2)[:, :, 0]
def fill(n, order, s):
    s = np.minimum(s, 16 - n[order]); c = np.add.accumulate(s); left = W - np.add.reduce(n); n = n.copy()
    n[order] = n[order] + np.clip(left - (c - s), 0, s)
    return n
def sizes(rng):
    a = (W // C) * rng.choice(np.array([0.5, 1.0, 1.5]))
    n = fill(np.zeros(C, np.int64), rng.permutation(C), 1 + rng.poisson(a, C))
    return fill(n, rng.permutation(C), np.full(C, 16))
def seat(rng, n):
    m = np.full((C, 16), W, np.int64); m[S16 < n[:, None]] = rng.permutation(W)
    return m
def seats(rng):
    return np.stack([np.stack([seat(rng, sizes(rng)) for g in range(8)]) for q in range(N)])
def people(rng, m):
    typ = rng.integers(0, 16, (8, 24, 16)); own = np.take_along_axis(rng.integers(0, 24, (8, C)), owner(m), 1)
    ty = np.where(rng.random((8, W)) < rng.choice(np.array([0.3, 0.7, 0.95]), (8, 1)), own, rng.integers(0, 24, (8, W)))
    v = typ[np.arange(8)[:, None], ty]
    return np.clip(v + rng.integers(-3, 4, (8, W, 16)), 0, 15)
def wrap(x, a, m, li, w):
    def turn(v): return np.ascontiguousarray(v.transpose(0, 1, 3, 2)).reshape(N, 128, -1)
    return {"x0": turn(x).astype(np.float32).astype(BF), "ac": turn(a).astype(np.int32), "ml": turn(m).astype(np.int32),
            "lims": np.repeat(li, 16, axis=1).astype(np.int32), "wt": w.reshape(N, 128, 1).astype(np.int32)}
def setup_inputs(rng):
    m = seats(rng); x = np.stack([people(rng, b) for b in m])
    li = np.stack([rng.integers(30, 130, (N, 8)), rng.integers(20, 110, (N, 8))], axis=2)
    return wrap(x, rng.integers(0, W, (N, 8, H, 16)), m, li, rng.integers(0, 256, (N, 8, 16)))
def setup_inputs_ends(rng):
    ms, xs, as_, ls = [], [], [], []
    for q in range(N):
        m = []
        for g in range(8):
            n = np.zeros(C, np.int64); n[:4] = 16; n[C - 4:] = 16; o = 4 + rng.permutation(C - 8)
            n = fill(n, o, rng.choice(np.array([1, 1, 1, 16, 16, 8]), C - 8)); n = fill(n, o, np.full(C - 8, 16)); b = seat(rng, n)
            c = C - 4 + (g + q) % 4
            for v, k in ((0, 0), (W - 1, 15)):
                at = np.argwhere(b == v)[0]; b[at[0], at[1]] = b[c, k]; b[c, k] = v
            m.append(b)
        m = np.stack(m); ty = rng.integers(0, 5, (8, C, 1, 1)); ty[:, :4] = 4; ty[:, C - 4:] = 4
        edge = ((S16 != 2) & (S16 != 15))[None, None, :, None]
        val = np.where(ty == 0, True, np.where(ty == 1, False, np.where(ty == 2, rng.random((8, C, 16, 1)) < 0.5, np.where(ty == 3, rng.random((8, C, 16, 16)) < 0.5, edge))))
        x = np.zeros((8, W + 1, 16), np.int64); x[np.arange(8)[:, None, None], m] = 15 * val
        far = rng.random((8, H, 16)) < np.where(rng.random((8, H, 1)) < 0.4, 1.1, 0.55)
        ms.append(m); xs.append(x[:, :W]); as_.append(np.where(far, (W - 1) * rng.integers(0, 2, (8, H, 16)), rng.integers(0, W, (8, H, 16))))
        ls.append(np.array([[0, 0], [0, 240], [240, 0], [240, 240]])[(np.arange(8) // 2 + q) % 4])
    w = 255 * rng.integers(0, 2, (N, 8, 16)); w[:, 3::4] = 255; w[:, 1] = 0
    return wrap(np.stack(xs), np.stack(as_), np.stack(ms), np.stack(ls), w)
def setup_inputs_corners(rng):
    ms, xs, as_, ls = [], [], [], []
    for q in range(N):
        m = []; l = []; x = rng.integers(0, 16, (8, W, 16))
        for g in range(8):
            k = (g + q) & 7; n = np.zeros(C, np.int64); o = rng.permutation(C); z = 4 * rng.permutation(L); u = o[(o & 3) != 0]
            if k < 2:
                n[z[:CAP + k]] = 16; n = fill(n, u, rng.choice(np.array([1, 4, 8, 16]), len(u))); n = fill(n, u, np.full(len(u), 16))
            elif k == 2: n[:] = W // C
            elif k == 3:
                n[:] = W // C; n[o[:3]] = 0; n[o[3:6]] = 2 * (W // C)
            elif k == 4:
                n[z[:L // 2]] = 8; n = fill(n, u, rng.choice(np.array([8, 9]), len(u)))
            elif k == 5: n = fill(n, o, np.full(C, 16))
            elif k == 6:
                n[z] = 1; n = fill(n, u, rng.choice(np.array([15, 16]), len(u)))
            else:
                n = sizes(rng); x[g] = rng.integers(0, 2, (W, 16))
            m.append(seat(rng, n)); l.append(((0, 240), (0, 240), (240, 0), (0, 0), (240, 240), (240, 0), (240, 0), (int(rng.integers(2, 14)), int(rng.integers(2, 9))))[k])
        m = np.stack(m); mb = owner(m); mode = rng.integers(0, 6, (8, H, 1)); a = rng.integers(0, W, (8, H, 16)); zero = []
        for g in range(8):
            c0 = np.nonzero((mb[g] & 3) == 0)[0]
            if len(c0) == 0: c0 = np.arange(W)
            zero.append(c0[rng.integers(0, len(c0), (H, 16))])
        a = np.where(mode == 1, a[:, :, :1], np.where(mode == 2, (W - 1) * rng.integers(0, 2, (8, H, 16)), np.where(mode == 3, np.arange(H)[None, :, None] + H * rng.integers(0, W // H, (8, H, 16)),
            np.where(mode == 4, np.stack(zero), np.where(mode == 5, a[:, :, S16 & 1], a)))))
        ms.append(m); xs.append(x); as_.append(a); ls.append(np.array(l))
    w = np.where(rng.random((N, 8, 16)) < 0.5, rng.integers(0, 256, (N, 8, 16)), rng.choice(np.array([0, 1, 255]), (N, 8, 16)))
    return wrap(np.stack(xs), np.stack(as_), np.stack(ms), np.stack(ls), w)
def setup_inputs_brim(rng):
    ms, xs, as_, ls = [], [], [], []
    for q in range(N):
        m = []; l = []; x = rng.integers(0, 16, (8, W, 16)); a = rng.integers(0, W, (8, H, 16))
        for g in range(8):
            k = (g + q) & 3; n = np.zeros(C, np.int64); o = rng.permutation(C); z = 4 * rng.permutation(L); u = o[(o & 3) != 0][:L]
            if k == 1:
                n[z] = 1; n[u] = 2; n = fill(n, o, rng.choice(np.array([0, 2, 4, 6]), C)); n = fill(n, o, 8 - n[o])
            else:
                n[z] = 4; n = fill(n, rng.permutation(np.concatenate([z, u])), rng.choice(np.array([0, 1, 4, 8, 12]), 2 * L)); n = fill(n, rng.permutation(z), np.full(L, 12))
            b = seat(rng, n)
            if k == 1:
                old = b[z, rng.integers(0, n[z])]; h = rng.permutation(H)[:L]; new = h + H * rng.integers(0, W // H, L); p = np.full(W + 1, W)
                p[old] = new; p[np.setdiff1d(np.arange(W), old)] = rng.permutation(np.setdiff1d(np.arange(W), new)); b = p[b]
                x[g] = rng.integers(1, 16, (W, 16)); x[g, new] = 0
                x[g, b[u, 0]] = np.where(S16 == rng.integers(0, 16, (L, 1)), 0, 12); x[g, b[u, 1]] = np.where(S16 == rng.integers(0, 16, (L, 1)), 1, 12)
                a[g, h] = np.where((rng.random((L, 16)) < 0.25) & (S16 > 1), new[rng.integers(0, L, (L, 16))], np.where((S16 & 1) == 1, b[u, 0][:, None], b[np.roll(u, -1), 1][:, None]))
            elif k == 2:
                p = np.argsort(rng.random((L, 16)), axis=1); j = np.argsort(rng.random((L, 4)), axis=1); x[g] = rng.integers(1, 10, (W, 16))
                x[g, b[z, j[:, 0]]] = 0; x[g, b[z, j[:, 1]]] = np.where(p < 10, 15, np.where(p == 10, 1, 0)); x[g, b[z, j[:, 2]]] = np.where(p >= 6, 15, np.where(p < 2, 1, 0))
            elif k == 3:
                ty = rng.integers(0, 3, (W, 1)); x[g] = np.where(ty == 0, 15, np.where((ty == 1) & (S16 == rng.integers(0, 16, (W, 1))), 1, 0))
            m.append(b); l.append(((0, 0), (240, 0), (0, 0), (0, 239 + (g >> 2)))[k])
        ms.append(np.stack(m)); xs.append(x); as_.append(a); ls.append(np.array(l))
    return wrap(np.stack(xs), np.stack(as_), np.stack(ms), np.stack(ls), rng.integers(0, 256, (N, 8, 16)))
def setup_inputs_ties(rng):
    m = seats(rng); two = np.array([[0, 1], [7, 8], [0, 15], [3, 6]])[(np.arange(8)[None, :] + np.arange(N)[:, None]) & 3]
    pool = rng.integers(0, 2, (N, 8, 12, 16)); pool = np.where(pool == 1, two[:, :, None, 1:], two[:, :, None, :1])
    kind = rng.integers(0, 12, (N, 8, W)); x = pool[np.arange(N)[:, None, None], np.arange(8)[None, :, None], kind]
    step = two[:, :, 1] - two[:, :, 0]; li = np.stack([step * rng.integers(5, 14, (N, 8)), step * rng.integers(3, 11, (N, 8))], axis=2)
    known = rng.integers(0, W, (N, 8, 40)); k = rng.integers(0, 40, (N, 8, H * 16))
    a = np.where(rng.random((N, 8, H, 1)) < 0.5, np.take_along_axis(known, k, 2).reshape(N, 8, H, 16), rng.integers(0, W, (N, 8, H, 16)))
    return wrap(x, a, m, np.minimum(li, 240), rng.integers(0, 256, (N, 8, 16)))
def setup_inputs_spread(rng):
    x = rng.integers(0, 2 ** rng.integers(0, 5, (N, 8, W, 1)), (N, 8, W, 16)); m = []
    for q in range(N):
        for g in range(8):
            n = fill(np.zeros(C, np.int64), rng.permutation(C), rng.choice(np.array([0, 1, 1, 2, 3, 5, 16]), C)); m.append(seat(rng, fill(n, rng.permutation(C), np.full(C, 16))))
    a = np.minimum((W * rng.random((N, 8, H, 16)) ** 3).astype(np.int64), W - 1); w = np.minimum((np.exp2(8 * rng.random((N, 8, 16))) - 1).astype(np.int64), 255)
    return wrap(x, a, np.stack(m).reshape(N, 8, C, 16), rng.integers(0, 241, (N, 8, 2)), w)
def check_inputs(d):
    bad = []
    for k, lo, hi in (("x0", 0, 15), ("ac", 0, W - 1), ("ml", 0, W), ("lims", 0, 240), ("wt", 0, 255)):
        a = np.asarray(d[k]).astype(np.float64)
        if not (np.min(a) >= lo and np.max(a) <= hi): bad.append("range of " + k)
    a = np.asarray(d["x0"]).astype(np.float64)
    if np.any(a != np.floor(a)): bad.append("whole numbers in x0")
    m = np.asarray(d["ml"]).astype(np.int64).reshape(N, 8, 16, C)
    if np.any(np.sort(m.reshape(N, 8, 16 * C), axis=-1) != np.minimum(np.arange(16 * C), W)): bad.append("every agent once in ml")
    if np.any((m[:, :, 1:] < W) & (m[:, :, :-1] >= W)): bad.append("members before empty slots in ml")
    l = np.asarray(d["lims"]).reshape(N, 8, 16, 2)
    if np.any(l != l[:, :, :1]): bad.append("lims alike in a group")
    return bad
def reference(x0, ac, ml, lims, wt):
    X = np.zeros((N, 8, W + 1, 16), np.int32)
    X[:, :, :W] = x0.astype(np.float32).astype(np.int32).reshape(N, 8, 16, W).transpose(0, 1, 3, 2)
    A = ac.reshape(N, 8, 16, H).transpose(0, 1, 3, 2); M = np.array(ml.reshape(N, 8, 16, C).transpose(0, 1, 3, 2))
    lim = lims.reshape(N, 8, 16, 2)[:, :, 0].astype(np.int64); wv = wt.reshape(N, 8, 16).astype(np.int64)
    G = np.arange(8)[:, None]; G3 = G[:, :, None]; low = np.tri(L, L, -1, dtype=bool); z = np.zeros(N, np.int64)
    for t in range(RO):
        cl = t & 3; lane = 4 * np.arange(L) + cl; M2 = M.copy(); X2 = X.copy(); z2 = np.zeros(N, np.int64); go = []
        for r in range(N):
            x, m, mb = X[r], M[r], owner(M[r])
            own = m[:, lane]; here = own < W; live = here[:, :, 0]; tx = x[G3, own]; U = np.max(tx, axis=2)
            gr = np.where(here, np.sum(U[:, :, None] - tx, axis=3), -1); s = pick(own, np.argmax(gr, axis=2)); xs = x[G, s]
            ds = np.where(here, np.sum((tx - xs[:, :, None]) ** 2, axis=3), -1)
            an = A[r][G, s & (H - 1)]; ad = mb[G3, an]; fit = live[:, :, None] & ((ad & 3) != cl); has = np.any(fit, axis=2)
            d = pick(ad, np.argmin(np.where(fit, np.sum((x[G3, an] - xs[:, :, None]) ** 2, axis=3), 2 ** 20), axis=2))
            first = ~np.any((d[:, :, None] == d[:, None, :]) & has[:, None, :] & low, axis=2)
            dm = m[G, d]; dh = dm < W; td = x[G3, dm]; V = np.maximum(U, np.max(td, axis=2))[:, :, None]
            worst = np.maximum(np.max(np.where(here, np.sum(V - tx, axis=3), 0), axis=2), np.max(np.where(dh, np.sum(V - td, axis=3), 0), axis=2))
            mer = has & first & (np.sum(here, axis=2) + np.sum(dh, axis=2) <= 16) & (worst <= lim[r, :, :1] + (z[r] & 15))
            want = live & ~mer & (np.max(gr, axis=2) > lim[r, :, 1:])
            xg = x[G, pick(own, np.argmax(ds, axis=2))]; away = here & (np.sum((tx - xg[:, :, None]) ** 2, axis=3) < ds)
            vacant = m[:, :, 0] >= W; free = np.argsort(~vacant, axis=1, kind="stable")
            k = np.add.accumulate(want.astype(np.int64), axis=1) - want.astype(np.int64)
            spl = want & (k < np.sum(vacant, axis=1)[:, None]); e = np.take_along_axis(free, k, 1)
            both = tight(np.concatenate([own, dm], axis=2))[:, :, :16]
            M2[r][:, lane] = np.where(mer[:, :, None], both, np.where(spl[:, :, None], tight(np.where(away, W, own)), own))
            a, b = np.nonzero(mer); M2[r][a, d[a, b]] = W
            a, b = np.nonzero(spl); M2[r][a, e[a, b]] = tight(np.where(away, own, W))[a, b]
            idle = live & ~mer & ~spl; a, b = np.nonzero(idle & (np.add.accumulate(idle.astype(np.int64), axis=1) <= CAP))
            go.append((a, s[a, b], xs[a, b])); z2[r] = np.sum(mer)
        for r in range(N):
            q = (r + 1 + t % (N - 1)) % N; a, sa, xa = go[r]
            v = np.sum(wv[q][a] * xa, axis=1) & (W - 1); mm = M2[q][a, owner(M2[q])[a, v]]; y = X[q][a[:, None], mm]
            j = np.argmin(np.where(mm < W, np.sum((y - xa[:, None]) ** 2, axis=2), 2 ** 20), axis=1)
            X2[r][a, sa] = (xa + y[np.arange(len(a)), j]) >> 1
        X, M, z = X2, M2, z2
    return {"ym": np.ascontiguousarray(M.transpose(0, 1, 3, 2)).reshape(N, 128, C).astype(np.float32),
            "yx": np.ascontiguousarray(X[:, :, :W].transpose(0, 1, 3, 2)).reshape(N, 128, W).astype(np.float32).astype(BF)}

@@ -1,0 +1,730 @@
+from concourse.mybir import AluOpType as A, ActivationFunctionType as F, AxisListType
+AX = AxisListType.X
+
+NX = 4368
+NO = 8576
+NE = 2064
+D0 = 4352
+BIG = float(2 ** 20)
+
+SCRATCH = {
+    "X": ("sbuf", [128, NX], "bfloat16"), "OW": ("sbuf", [128, NO], "float32"), "AC": ("sbuf", [128, NX], "int32"),
+    "ML": ("sbuf", [128, 1280], "float32"), "MI": ("sbuf", [128, 1280], "int32"), "TB": ("sbuf", [128, NE + 1280], "bfloat16"),
+    "TX": ("sbuf", [128, 4096], "bfloat16"), "US": ("sbuf", [128, 4096], "bfloat16"), "XE": ("sbuf", [128, 4096], "bfloat16"),
+    "XSE": ("sbuf", [128, 4096], "bfloat16"), "DF": ("sbuf", [128, 4096], "bfloat16"), "OWG": ("sbuf", [128, 4096], "bfloat16"),
+    "SQO": ("sbuf", [128, 4096], "bfloat16"), "SQ": ("sbuf", [128, 4096], "bfloat16"), "PR": ("sbuf", [128, 4096], "bfloat16"),
+    "TD": ("sbuf", [128, 4096], "bfloat16"), "UD": ("sbuf", [128, 4096], "bfloat16"), "VAL": ("sbuf", [128, 4096], "float32"),
+    "NWE": ("sbuf", [128, 4096], "bfloat16"), "RM": ("sbuf", [128, 4096], "bfloat16"),
+    "XS": ("sbuf", [128, 256], "bfloat16"), "ONE": ("sbuf", [128, 128], "float32"), "ONEB": ("sbuf", [128, 128], "bfloat16"), "IDF": ("sbuf", [128, 128], "float32"),
+    "IDK": ("sbuf", [128, 128], "float32"), "IDB": ("sbuf", [128, 128], "bfloat16"), "NID": ("sbuf", [128, 128], "bfloat16"),
+    "IDV": ("sbuf", [128, 128], "bfloat16"), "BO": ("sbuf", [128, 128], "bfloat16"), "G16": ("sbuf", [128, 8], "bfloat16"),
+    "G64": ("sbuf", [128, 8], "bfloat16"), "G2": ("sbuf", [128, 8], "bfloat16"), "GM2": ("sbuf", [128, 8], "bfloat16"),
+    "GS0": ("sbuf", [128, 8], "bfloat16"), "GS0F": ("sbuf", [128, 8], "float32"), "GD": ("sbuf", [128, 8], "bfloat16"), "GC": ("sbuf", [128, 32], "bfloat16"),
+    "QM": ("sbuf", [128, 1024], "float32"), "QI": ("sbuf", [128, 1280], "int32"), "QJ": ("sbuf", [128, 1280], "int32"),
+    "RB": ("sbuf", [128, 8], "float32"), "BM": ("sbuf", [128, 256], "bfloat16"), "ROW": ("sbuf", [128, 1024], "bfloat16"),
+    "WQ": ("sbuf", [128, 2048], "bfloat16"), "WT": ("sbuf", [128, 2048], "bfloat16"), "BOX": ("sbuf", [128, 8, 32], "bfloat16"),
+    "IXA": ("sbuf", [128, 8, 32], "float32"), "IXB": ("sbuf", [128, 8, 32], "float32"), "TRI": ("sbuf", [128, 128], "bfloat16"),
+    "TRJ": ("sbuf", [128, 128], "bfloat16"), "DUM": ("sbuf", [128, 256], "float32"), "CO": ("sbuf", [128, 256], "float32"),
+    "CI": ("sbuf", [128, 64], "float32"), "RW1": ("sbuf", [128, 512], "bfloat16"), "RW2": ("sbuf", [128, 512], "bfloat16"),
+    "LMI": ("sbuf", [128, 2], "int32"), "WTI": ("sbuf", [128, 1], "int32"), "LMF": ("sbuf", [128, 8], "float32"), "LIM": ("sbuf", [128, 64], "float32"),
+    "OFO": ("sbuf", [128, 256], "uint16"), "ACO": ("sbuf", [128, 256], "uint16"), "OFD": ("sbuf", [128, 256], "uint16"),
+    "MVO": ("sbuf", [128, 256], "uint16"), "LST": ("sbuf", [128, 512], "uint16"), "HL": ("sbuf", [128, 64], "uint16"),
+    "IND": ("sbuf", [128, 1024], "bfloat16"), "INDD": ("sbuf", [128, 256], "bfloat16"),
+    "K1": ("sbuf", [128, 256], "float32"), "KM": ("sbuf", [128, 256], "float32"), "KB": ("sbuf", [128, 256], "float32"),
+    "KD": ("sbuf", [128, 256], "float32"), "KA": ("sbuf", [128, 256], "float32"), "MSD": ("sbuf", [128, 256], "float32"),
+    "E1": ("sbuf", [128, 1024], "float32"), "EM": ("sbuf", [128, 1024], "float32"), "EX": ("sbuf", [128, 256], "float32"),
+    "E2": ("sbuf", [128, 512], "float32"), "TH": ("sbuf", [128, 512], "float32"), "EQ": ("sbuf", [128, 256], "float32"), "DS": ("sbuf", [128, 256], "float32"),
+    "SM": ("sbuf", [128, 1024], "float32"), "SI": ("sbuf", [128, 256], "int32"), "SB": ("sbuf", [128, 64], "bfloat16"),
+    "OCB": ("sbuf", [128, 64], "bfloat16"), "CF": ("sbuf", [128, 768], "bfloat16"), "FS": ("sbuf", [128, 512], "float32"),
+    "XB": ("sbuf", [128, 256], "bfloat16"), "PS": ("sbuf", [128, 512], "bfloat16"), "VM": ("sbuf", [128, 256], "bfloat16"),
+    "MD": ("sbuf", [128, 256], "float32"), "TG": ("sbuf", [128, 256], "bfloat16"), "PRS": ("sbuf", [128, 512], "float32"),
+    "W": ("sbuf", [128, 16, 32], "float32"), "H3": ("sbuf", [128, 16, 32], "float32"), "ZI": ("sbuf", [128, 512], "int32"),
+    "F1": ("sbuf", [128, 16, 16], "float32"), "F2": ("sbuf", [128, 16, 16], "float32"), "L2": ("sbuf", [128, 256], "float32"),
+    "VS": ("sbuf", [128, 336], "bfloat16"), "XVE": ("sbuf", [128, 1024], "bfloat16"), "XVS": ("sbuf", [128, 1024], "bfloat16"),
+    "VD": ("sbuf", [128, 1024], "bfloat16"), "SQV": ("sbuf", [128, 1024], "bfloat16"), "OVG": ("sbuf", [128, 64], "bfloat16"),
+    "RET": ("sbuf", [128, 64], "bfloat16"), "NX1": ("sbuf", [128, 256], "bfloat16"),
+}
+WIDTH = {k: v[1][1] for k, v in SCRATCH.items()}
+SHARE = {"SQ": "DF", "PR": "XSE", "TD": "SQO", "UD": "OWG", "NWE": "XE", "XVS": "XE", "E2": "E1", "FS": "TH", "KA": "K1", "MSD": "KM",
+         "L2": "MD", "ZI": "QI", "SQV": "SQO", "QJ": "MI"}
+for _k in SHARE:
+    del SCRATCH[_k]
+for _t in range(4):
+    WIDTH["XV%d" % _t] = 64
+    WIDTH["ME%d" % _t] = 336
+    SCRATCH["XV%d" % _t] = ("sbuf", [128, 64], "bfloat16")
+    SCRATCH["ME%d" % _t] = ("sbuf", [128, 336], "bfloat16")
+for _b in range(8):
+    WIDTH["B%d" % _b] = 512
+    SCRATCH["B%d" % _b] = ("psum", [128, 512], "float32")
+SEMAPHORES = ["v", "s", "p", "gg", "dx", "da", "dm", "dl", "dw", "oy", "ox"] + ["%s%d" % (a, b) for a in ("va", "vl", "ra", "rl") for b in range(4)]
+PSUM = ["B%d" % b for b in range(8)]
+SIZE = {"float32": 4, "int32": 4, "bfloat16": 2, "uint16": 2}
+
+
+def rank_program(g, core, T, topo):
+    rank = T.rank_of(core)
+    if rank is None:
+        return
+    n = len(T.cores)
+    queue = {"v": g.vector, "s": g.scalar, "p": g.tensor, "gg": g, "y": g.sync}
+    count = {}
+    known = {q: {} for q in queue}
+    clock = {}
+    log = {}
+
+    def R(b, lo=0, hi=None, st=1, p0=0, p1=128):
+        hi = WIDTH[b] if hi is None else min(hi, WIDTH[b])
+        b = SHARE.get(b, b)
+        full = p0 == 0 and p1 == 128
+        ap = T[b][:, lo:hi:st] if full else T[b][p0:p1, lo:hi:st]
+        return (ap, [(b, lo, hi, st)])
+
+    def R3(b, a0, a1, k0, k1):
+        s = SCRATCH[b][1][2]
+        return (T[b][:, a0:a1, k0:k1], [(b, a0 * s, a1 * s, 1)])
+
+    def I(b, lo, hi, ob, o0, o1):
+        b, ob = SHARE.get(b, b), SHARE.get(ob, ob)
+        return (T[b][:, lo:hi].indirect(T[ob][:, o0:o1]), [(b, lo, hi, 1), (ob, o0, o1, 1)])
+
+    def need(q, reads, writes, dma=False):
+        out = []
+        for regs, w in ((reads, False), (writes, True)):
+            for (b, lo, hi, st) in regs:
+                ps = b in PSUM
+                if dma and w:
+                    al = 16 // SIZE[SCRATCH[b][2]]
+                    lo, hi, st = lo // al * al, -(-hi // al) * al, 1
+                for (l2, h2, s2, w2, e, c, d2) in log.get(b, []):
+                    if ps:
+                        if e == q and (q == "p" or not (w or w2) or lo >= h2 or l2 >= hi):
+                            continue
+                    else:
+                        if not (w or w2):
+                            continue
+                        if d2 and w2 and w:
+                            al = 16 // SIZE[SCRATCH[b][2]]
+                            l2, h2, s2 = l2 // al * al, -(-h2 // al) * al, 1
+                        if lo >= h2 or l2 >= hi or (st == s2 and st > 1 and (lo - l2) % st):
+                            continue
+                    out.append((e, c))
+        best = {}
+        for e, c in out:
+            best[e] = max(best.get(e, 0), c)
+        for e, c in sorted(best.items(), key=lambda x: -x[1]):
+            if known[q].get(e, 0) < c:
+                queue[q].wait_ge(T.sem[e], c)
+                for k, v in clock[(e, c)].items():
+                    known[q][k] = max(known[q].get(k, 0), v)
+
+    def done(q, e, inc, reads, writes, dma=False):
+        count[e] = count.get(e, 0) + inc
+        c = count[e]
+        ck = dict(known[q])
+        ck[e] = c
+        clock[(e, c)] = ck
+        for (b, lo, hi, st) in writes:
+            keep = [r for r in log.get(b, []) if not (b not in PSUM and st == 1 and lo <= r[0] and r[1] <= hi)]
+            log[b] = keep + [(lo, hi, st, True, e, c, dma)]
+        for (b, lo, hi, st) in reads:
+            l = log.setdefault(b, [])
+            l[:] = [r for r in l if not (r[:4] == (lo, hi, st, False) and r[4] == e)]
+            l.append((lo, hi, st, False, e, c, dma))
+        if len(log) and any(b in PSUM for (b, _a, _b, _c) in reads + writes):
+            for b in set(x[0] for x in reads + writes if x[0] in PSUM):
+                if len(log[b]) > 60:
+                    m = {}
+                    for r in log[b]:
+                        k = (r[4], r[3])
+                        o = m.get(k)
+                        m[k] = r if o is None else (min(o[0], r[0]), max(o[1], r[1]), 1, r[3], r[4], max(o[5], r[5]), r[6])
+                    log[b] = list(m.values())
+
+    def op(q, f, out, ins):
+        rd = [x for i in ins if isinstance(i, tuple) for x in i[1]]
+        wr = list(out[1])
+        if len(wr) > 1:
+            rd = rd + wr[1:]
+            wr = wr[:1]
+        need(q, rd, wr)
+        f().then_inc(T.sem[q], 1)
+        done(q, q, 1, rd, wr)
+
+    def ap(x):
+        return x[0] if isinstance(x, tuple) else x
+
+    def tc(o, i):
+        op("v", lambda: g.vector.tensor_copy(o[0], i[0]), o, [i])
+
+    def tt(o, a, b, f):
+        op("v", lambda: g.vector.tensor_tensor(o[0], a[0], b[0], f), o, [a, b])
+
+    def ts(o, a, s1, f1, s2=None, f2=None):
+        if f2 is None:
+            op("v", lambda: g.vector.tensor_scalar(o[0], a[0], ap(s1), None, f1), o, [a, s1])
+        else:
+            op("v", lambda: g.vector.tensor_scalar(o[0], a[0], ap(s1), ap(s2), f1, f2), o, [a, s1, s2])
+
+    def ms(o, c):
+        op("v", lambda: g.vector.memset(o[0], c), o, [])
+
+    def scan(o, d0, d1, f0, f1, init=0.0):
+        op("v", lambda: g.vector.tensor_tensor_scan(o[0], d0[0], d1[0], init, f0, f1), o, [d0, d1])
+
+    def act(o, i, f, **kw):
+        op("s", lambda: g.scalar.activation(o[0], i[0], f, **kw), o, [i])
+
+    def mm(o, l, r, a, z):
+        op("p", lambda: g.tensor.matmul(o[0], l[0], r[0], a, z), o, [l, r])
+
+    def aff(o, i, pat, cmp, fill, base, cm):
+        op("gg", lambda: g.affine_select(o[0], i[0], pat, cmp, fill, base, cm), o, [i])
+
+    def iota(o, pat, base, cm, **kw):
+        op("gg", lambda: g.iota(o[0], pat, base, cm, **kw), o, [])
+
+    def dma(q, sem, o_ap, i_ap, reads, writes):
+        need(q, reads, writes, True)
+        queue[q].dma_start(o_ap, i_ap).then_inc(T.sem[sem], 16)
+        done(q, sem, 16, reads, writes, True)
+
+    def fin(q, sem):
+        if known[q].get(sem, 0) < count[sem]:
+            queue[q].wait_ge(T.sem[sem], count[sem])
+
+    def send(dst, ob, osz, ib, rs, ls):
+        eng = topo.engines(core, T.cores[dst])[:4]
+        mask = sum(1 << e for e in eng)
+        rid, pid, _se = topo.addr(T.cores[dst])
+        i = R(ib, 0, 64)
+        need("gg", i[1], [])
+        g.remote_dma(T[ob][:, 0:64], i[0], T.sem[rs], T.sem[ls], pid, rid, mask)
+        done("gg", ls, len(eng), i[1], [])
+
+    def arrive(sem, b):
+        count[sem] = 4
+        clock[(sem, 4)] = {sem: 4}
+        log.setdefault(b, []).append((0, 64, 1, True, sem, 4, True))
+
+    def bounded(o, pat, base, cm, width):
+        aff(o, o, pat, A.is_ge, 0.0, base, cm)
+        aff(o, o, [[-s, k] for s, k in pat], A.is_ge, 0.0, width - 1 - base, -cm)
+
+    ms(R("X", 0, 16), -16.0)
+    ms(R("X", 4096, NX), 0.0)
+    ms(R("AC", 0, 8), 0)
+    ms(R("AC", 4096, NX), 0)
+    mi = R("MI", 0, 1024)
+    dma("y", "dm", mi[0], T.ml[:, :], [], mi[1])
+    dma("y", "dx", T.X[:, 1:4097], T.x0[:, :], [], R("X", 1, 4097)[1])
+    for j in range(4):
+        dma("y", "da", T.AC[:, 1 + 1024 * j:1025 + 1024 * j], T.ac[:, :], [], R("AC", 1 + 1024 * j, 1025 + 1024 * j)[1])
+    for b in ("AC",):
+        log[b] = [r[:5] + (64,) + r[6:] if r[4] == "da" else r for r in log[b]]
+    dma("y", "dl", T.LMI[:], T.lims[:, :], [], R("LMI")[1])
+    dma("y", "dw", T.WTI[:], T.wt[:, :], [], R("WTI")[1])
+    one = R("ONE", 0, 128)
+    ms(R("ONE"), 1.0)
+    iota(R("QI", 0, 1024), [[0, 64], [-1, 16]], 1024, 1)
+    ms(R("VAL"), 1.0)
+    aff(R("IDF"), one, [[-1, 128]], A.is_equal, 0.0, 0, 1)
+    iota(R("DUM"), [[16, 256]], D0, 1, allow_small_or_imprecise_dtypes=True)
+    ms(R("ML", 1024, 1280), 0.0)
+    ts(R("ML", 0, 1024), mi, 4096, A.is_equal, -4097, A.mult)
+    tt(R("ML", 0, 1024), R("ML", 0, 1024), mi, A.add)
+    ts(R("ML", 0, 1024), R("ML", 0, 1024), 1, A.add)
+    iota(R("QJ"), [[1, 1280]], 0, 0)
+    ts(R("QI", 0, 1024), R("QI", 0, 1024), 15, A.bitwise_and)
+    ts(R("QM"), R("QI", 0, 1024), 0, A.is_equal)
+    q_ = lambda k: R("QM", k, k + 1)
+
+    def tmp(o, w, pats, src=None):
+        t = R("VAL", o, o + w)
+        for p in pats:
+            bounded(t, *p)
+        return t
+    bo = tmp(0, 128, [([[-16, 8], [0, 16]], 0, 1, 16)])
+    tc(R("BO"), bo)
+    rb = tmp(128, 8, [([[-16, 8]], 0, 1, 16)])
+    tc(R("RB"), rb)
+    tri = tmp(256, 128, [([[1, 128]], -1, -1, 200)])
+    tc(R("TRI"), tri)
+    trj = tmp(384, 128, [([[1, 128]], 0, -1, 200)])
+    tc(R("TRJ"), trj)
+    sel = R("VAL", 2048, 4096)
+    aff(sel, sel, [[1, 16], [0, 8], [-1, 16]], A.is_equal, 0.0, 0, 0)
+    bounded(sel, [[0, 16], [-16, 8], [0, 16]], 0, 1, 16)
+    tc(R("ONEB"), one)
+    tc(R("IDB"), R("IDF"))
+    ts(R("NID"), R("IDF"), -1.0, A.mult)
+    ts(R("IDK"), R("IDF"), 1024.0, A.mult)
+    ts(R("IDV"), R("IDF"), float(2 ** 18), A.mult)
+    g8 = R("BO", 0, 128, 16)
+    for b, c in (("G16", 16.0), ("G64", 65536.0), ("G2", 2.0), ("GM2", -2.0)):
+        ts(R(b), g8, c, A.mult)
+    ts(R("GS0"), g8, q_(0), A.mult)
+    ts(R("GS0F"), g8, q_(0), A.mult)
+    wc = R("SM", 0, 1)
+    ts(wc, q_(0), 128.0, A.mult)
+    tt(wc, wc, q_(1), A.add)
+    ts(R("SM", 1, 2), q_(6), -129.0, A.mult)
+    tt(wc, wc, R("SM", 1, 2), A.add)
+    ts(R("GD"), g8, wc, A.mult)
+    for u in range(4):
+        tt(R("SM", 2, 3), q_(2 + u), q_(6), A.subtract)
+        ts(R("GC", 8 * u, 8 * u + 8), g8, R("SM", 2, 3), A.mult, float(2 ** 17), A.mult)
+    ts(R("WQ"), sel, wc, A.mult)
+    tc(R("SM", 3, 4), R("WTI"))
+    ts(R("WT"), sel, R("SM", 3, 4), A.mult)
+    ms(R("RM"), 1.0)
+    ms(R("RM", 0, 4096, 16), 0.0)
+    ms(R("BM"), 0.0)
+    ms(R("BM", 0, 256, 16), float(2 ** 25))
+    for b, s in (("RW1", 128), ("RW2", 256)):
+        ms(R(b), 1.0)
+        ms(R(b, 0, 512, s), 0.0)
+    iota(R("EM", 0, 128), [[0, 8], [4096, 16]], 0, 0, allow_small_or_imprecise_dtypes=True)
+    iota(R("EM", 128, 256), [[0, 8], [1, 16]], 0, 0, allow_small_or_imprecise_dtypes=True)
+    iota(R("EM", 256, 384), [[0, 8], [-1, 16]], 15, 0, allow_small_or_imprecise_dtypes=True)
+    iota(R("EM", 512, 768), [[-1, 256]], 0, 0, allow_small_or_imprecise_dtypes=True)
+    tc(R("ROW", 0, 384), R("EM", 0, 384))
+    ms(R("ROW", 384, 512), -1.0)
+    tc(R("ROW", 512, 768), R("EM", 512, 768))
+    row = lambda a, w: R("ROW", a, a + w, 1, 0, 1)
+    lone = R("ONEB", 0, 128, 1, 0, 1)
+    b3 = R("BO", 0, 128)
+    ts(R3("BOX", 0, 8, 0, 16), b3, -1.0, A.mult)
+    tc(R3("BOX", 0, 8, 16, 32), b3)
+    ms(R3("IXA", 0, 8, 16, 32), 0.0)
+    ms(R3("IXB", 0, 8, 0, 16), 0.0)
+    ts(R3("IXA", 0, 8, 0, 16), R("IDF"), 2.0 ** -10, A.mult)
+    ts(R3("IXB", 0, 8, 16, 32), R("IDF"), 2.0 ** -10, A.mult)
+    ms((T.W[:, :, :], [("W", 0, 512, 1)]), 0.0)
+    w2 = lambda: (T.W[:, :, :], [("W", 0, 512, 1)])
+    ms(R3("W", 0, 16, 16, 32), -1.0)
+    tc(R("ROW", 768, 1024), (T.W[:, 0:8, :], [("W", 0, 512, 1)]))
+    C = lambda a: R("CO", 16 * a, 16 * a + 16)
+    iota(C(0), [[128, 2], [0, 8]], 4097, 1, allow_small_or_imprecise_dtypes=True)
+    iota(C(1), [[2048, 2], [0, 8]], 15, 16, allow_small_or_imprecise_dtypes=True)
+    iota(C(2), [[-128, 2], [0, 8]], 4096, -1, allow_small_or_imprecise_dtypes=True)
+    iota(C(3), [[128, 2], [0, 8]], NE + 1024, 1, allow_small_or_imprecise_dtypes=True)
+    iota(C(4), [[128, 2], [0, 8]], 64, 1, allow_small_or_imprecise_dtypes=True)
+    iota(C(5), [[0, 16]], 0, 16, allow_small_or_imprecise_dtypes=True)
+    for t in range(4):
+        iota(C(6 + t), [[512, 2], [0, 8]], t, 4, allow_small_or_imprecise_dtypes=True)
+        iota(C(10 + t), [[512, 2], [0, 8]], t + NE, 4, allow_small_or_imprecise_dtypes=True)
+    iota(R("CI"), [[128, 8], [0, 8]], 0, 1, allow_small_or_imprecise_dtypes=True)
+    pl = R("TB", NE, NE + 1280)
+    t1, t2 = R("VAL", 0, 1280), R("QI")
+    ts(t2, R("QJ"), 7, A.logical_shift_right)
+    ts(t1, t2, q_(0), A.mult, 128.0, A.add)
+    ts(t2, R("QJ"), 127, A.bitwise_and)
+    ts(R("E1", 0, 1024), R("QI", 0, 1024), q_(1), A.mult)
+    ts(R("EM", 0, 256), R("QI", 1024, 1280), q_(1), A.mult)
+    tt(R("VAL", 0, 1024), R("VAL", 0, 1024), R("E1", 0, 1024), A.add)
+    tt(R("VAL", 1024, 1280), R("VAL", 1024, 1280), R("EM", 0, 256), A.add)
+    ts(t2, R("QJ"), 3, A.bitwise_and)
+    ms(R("SM", 4, 6), 0.0)
+    for u in range(4):
+        ts(R("SM", 6, 7), q_(2 + u), float(u), A.mult)
+        tt(R("SM", 4, 5), R("SM", 4, 5), R("SM", 6, 7), A.add)
+        tt(R("SM", 5, 6), R("SM", 5, 6), q_(2 + u), A.add)
+    ts(R("E1", 0, 1024), R("QI", 0, 1024), R("SM", 4, 5), A.is_equal, R("SM", 5, 6), A.mult)
+    ts(R("EM", 0, 256), R("QI", 1024, 1280), R("SM", 4, 5), A.is_equal, R("SM", 5, 6), A.mult)
+    tt(R("TB", NE, NE + 1024), R("VAL", 0, 1024), R("E1", 0, 1024), A.add)
+    tt(R("TB", NE + 1024, NE + 1280), R("VAL", 1024, 1280), R("EM", 0, 256), A.add)
+    ms(R("TB", 0, NE), 128.0)
+    for k in range(11):
+        ms(R("SM", 16 + k, 17 + k), float(2 ** (10 - k)))
+    ms(R("SM", 27, 32), 0.0)
+    tt(R("SM", 16, 32), R("SM", 16, 32), R("QM", 0, 16), A.mult)
+    op("v", lambda: g.vector.tensor_reduce(T.LMF[:, 0:1], T.SM[:, 16:32], AX, A.add), R("LMF", 0, 1), [R("SM", 16, 32)])
+    iota(R("SI", 0, 1), [[0, 1]], 0, 1)
+    ts(R("SI", 0, 1), R("SI", 0, 1), 16, A.bitwise_and)
+    ts(R("LMF", 1, 2), R("SI", 0, 1), 16.0, A.is_equal)
+    ts(R("LMF", 2, 3), R("LMF", 1, 2), -1.0, A.mult, 1.0, A.add)
+    ts(R("LMF", 3, 4), R("LMF", 1, 2), 1 / 32, A.mult)
+    ts(R("LMF", 4, 5), R("LMF", 1, 2), -16.0, A.mult)
+    ts(R("LMF", 5, 6), R("LMF", 2, 3), 1 / 32, A.mult)
+    ts(R("LMF", 6, 7), R("LMF", 2, 3), -16.0, A.mult)
+    tc(R("SM", 8, 10), R("LMI"))
+    for j in range(2):
+        ts(R("K1", 0, 128), one, R("SM", 8 + j, 9 + j), A.mult)
+        for h in range(2):
+            mm(R("B0", 16 * j + 8 * h, 16 * j + 8 * h + 8), R("K1", 0, 128), R("GS0F"), True, True)
+    tc(R("LIM", 0, 32), R("B0", 0, 32))
+    tc(R("LIM", 32, 48), R("LIM", 0, 16))
+    for b, v in (("XE", 0.0), ("NWE", 0.0), ("E1", 0.0), ("E2", 0.0), ("VS", 0.0), ("XVS", 0.0)):
+        ms(R(b), v)
+    for t in range(4):
+        ms(R("ME%d" % t, 64, 336), 0.0)
+    ms(R("OW", 0, 16), 128.0)
+
+    def wrap(cols, e0, lo, bank, ps, keep=None):
+        w = 16 * cols
+        x = keep if keep is not None else R(ps, 0, w)
+        scan(x, R("RM", 0, w), R("E1", e0, e0 + w), A.mult, A.add)
+        tt(R("EM", 0, w), x, R("QM", 0, w), A.mult)
+        for h in range(cols // 8):
+            mm(R(bank, 8 * h, 8 * h + 8), R("EM", 128 * h, 128 * h + 128), R("RB"), True, True)
+        return R(bank, 0, cols)
+
+    def moved(ids, b):
+        ts(R("EQ"), ids, 0.0, A.is_equal)
+        tt(R("EQ"), R("EQ"), R("DUM"), A.mult)
+        tt(R("EQ"), R("EQ"), ids, A.add)
+        tc(R(b), R("EQ"))
+
+    def owners(b):
+        moved(R("ML", 256 * b, 256 * b + 256), "MVO")
+        tc(R("NWE", 0, 4096, 16), R("TB", NE + 256 * b, NE + 256 * b + 256))
+        scan(R("VAL"), R("RM"), R("NWE"), A.mult, A.add)
+        act(I("OW", 0, NO, "MVO", 0, 256), R("VAL"), F.Silu)
+
+    S = lambda a, w=16: R("SM", 16 * a, 16 * a + w)
+    NN, LIVE, HAS, FM, DD, MS, GR, WAN, SPL, RK, IDL, VIS, T1, T2, RV = range(4, 19)
+    SUU, S1, NV, NM, AA = 20, 21, 22, 23, 24
+
+    for t in range(4):
+        cl = t & 3
+        own = lambda h, b="ML": R(b, cl + 512 * h, cl + 512 * h + 512, 4)
+        tc(R("OFO"), R("ML", cl, 1024, 4))
+        tc(R("TX", 0, 2048), I("X", 0, NX, "OFO", 0, 128))
+        act(R("TX", 2048, 4096), I("X", 0, NX, "OFO", 128, 256), F.Copy)
+        ts(R("IND"), R("ML", 0, 1024), 0.0, A.is_gt)
+        for h in range(2):
+            o = R("B0", 128 * h, 128 * h + 128)
+            mm(o, own(h), R("IDF"), True, False)
+            mm(o, lone, row(0, 128), False, False)
+            mm(o, lone, row(384, 128), False, False)
+            for k in range(16):
+                mm(R("B0", 128 * h + k, 128 * h + 128, 16), R("TX", 2048 * h + k, 2048 * h + 2048, 16), R("G64"), False, k == 15)
+        act(R("K1"), R("B0", 0, 256), F.Abs)
+        for h in range(2):
+            mm(R("B1", 8 * h, 8 * h + 8), own(h, "IND"), g8, True, True)
+        scan(R("US", 0, 2048), R("RM", 0, 2048), R("TX", 0, 2048), A.mult, A.max)
+        scan(R("KM"), R("BM"), R("K1"), A.max, A.min)
+        tc(S(NN), R("B1", 0, 16))
+        ts(S(LIVE), S(NN), 0.0, A.is_gt)
+        tc(R("SI", 0, 16), R("KM", 15, 256, 16))
+        ts(R("SI", 16, 32), R("SI", 0, 16), 4095, A.bitwise_and)
+        ts(R("SI", 32, 48), R("SI", 0, 16), 16, A.logical_shift_right)
+        ts(S(T1), R("SI", 16, 32), 1.0, A.add)
+        tt(S(T1), S(T1), C(0), A.subtract)
+        tt(S(T1), S(T1), S(LIVE), A.mult)
+        tt(R("E1", 0, 256, 16), S(T1), C(0), A.add)
+        w = wrap(16, 0, 0, "B2", "B3")
+        tc(R("LST", 0, 16), w)
+        tc(R("XE", 0, 4096, 16), I("X", 0, NX, "LST", 0, 16))
+        ts(R("ACO"), I("AC", 0, NX, "LST", 0, 16), 1, A.add)
+        xs = R("XS")
+        tc(xs, R("XE", 0, 4096, 16))
+        scan(R("XSE"), R("RM"), R("XE"), A.mult, A.add)
+        for kk in range(8):
+            b = ("B4", "B5", "B6")[kk % 3]
+            for j in range(2):
+                o = R(b, 256 * j, 256 * j + 256)
+                mm(o, R("IDB"), R("TX", 2 * kk + j, 4096, 16), True, False)
+                mm(o, R("NID"), xs, False, True)
+            act(R("SQO", 512 * kk, 512 * kk + 512), R(b), F.Square)
+        if t == 0:
+            for b in range(4):
+                owners(b)
+        for h in range(2):
+            act(R("OWG", 2048 * h, 2048 * h + 2048), I("OW", 0, NO, "ACO", 128 * h, 128 * h + 128), F.Copy)
+        scan(R("US", 2048, 4096), R("RM", 2048, 4096), R("TX", 2048, 4096), A.mult, A.max)
+        for h in range(2):
+            mm(R("B1", 16 + 8 * h, 24 + 8 * h), R("US", 2048 * h + 15, 2048 * h + 2048, 16), g8, True, True)
+        for h in range(2):
+            o = R("B3", 128 * h, 128 * h + 128)
+            mm(o, own(h, "IND"), R("IDV"), True, False)
+            mm(o, lone, row(256, 128), False, False)
+            for k in range(16):
+                mm(R("B3", 128 * h + k, 128 * h + 128, 16), R("SQO", 256 * k + 128 * h, 256 * k + 128 * h + 128), R("G16"), False, k == 15)
+        for h in range(2):
+            tt(R("DF", 2048 * h, 2048 * h + 2048), I("X", 0, NX, "ACO", 128 * h, 128 * h + 128), R("XSE", 2048 * h, 2048 * h + 2048), A.subtract)
+            act(R("SQ", 2048 * h, 2048 * h + 2048), R("DF", 2048 * h, 2048 * h + 2048), F.Square)
+        tc(S(SUU), R("B1", 16, 32))
+        scan(R("KB"), R("RM", 0, 256), R("B3", 0, 256), A.mult, A.max)
+        tc(R("SI", 48, 64), R("KB", 15, 256, 16))
+        ts(R("SI", 48, 64), R("SI", 48, 64), 15, A.bitwise_and)
+        tt(R("E1", 0, 256, 16), C(1), R("SI", 48, 64), A.subtract)
+        w = wrap(16, 0, 0, "B2", "B3")
+        tc(R("LST", 16, 32), w)
+        tc(R("XB"), I("TX", 0, 4096, "LST", 16, 32))
+        mm(R("B4", 0, 256), R("IDB"), xs, True, False)
+        mm(R("B4", 0, 256), R("NID"), R("XB"), False, True)
+        for h in range(2):
+            o = R("B0", 128 * h, 128 * h + 128)
+            mm(o, lone, row(128, 128), True, False)
+            for k in range(16):
+                c = R("B0", 128 * h + k, 128 * h + 128, 16)
+                mm(c, R("OWG", 2048 * h + k, 2048 * h + 2048, 16), R("GC", 8 * cl, 8 * cl + 8), False, False)
+                mm(R("B5", 128 * h + k, 128 * h + 128, 16), R("OWG", 2048 * h + k, 2048 * h + 2048, 16), R("GD"), True, True)
+            for k in range(16):
+                mm(R("B0", 128 * h + k, 128 * h + 128, 16), R("SQ", 2048 * h + k, 2048 * h + 2048, 16), R("G16"), False, k == 15)
+        tt(R("PS", 0, 256), xs, R("B4", 0, 256), A.mult)
+        tt(R("PS", 256, 512), R("XB"), R("B4", 0, 256), A.mult)
+        for k in range(4):
+            tt(R("PR", 256 * k, 256 * k + 256), R("TX", k, 4096, 16), R("B4", 0, 256), A.mult)
+        scan(R("KD"), R("BM"), R("B0", 0, 256), A.max, A.min)
+        tc(R("E1", 0, 256, 16), R("KD", 15, 256, 16))
+        scan(R("EX"), R("RM", 0, 256), R("E1", 0, 256), A.mult, A.add)
+        tt(R("EQ"), R("EX"), R("B0", 0, 256), A.is_equal)
+        tt(R("EQ"), R("EQ"), R("B5", 0, 256), A.mult)
+        scan(R("DS"), R("RM", 0, 256), R("EQ"), A.mult, A.add)
+        ts(S(HAS), R("KD", 15, 256, 16), float(2 ** 17), A.is_lt)
+        tt(S(HAS), S(HAS), S(LIVE), A.mult)
+        ts(S(T1), R("DS", 15, 256, 16), float(-cl), A.add)
+        tt(S(T1), S(T1), S(HAS), A.mult)
+        ts(S(DD), S(T1), float(cl), A.add)
+        tc(R("E1", 0, 256, 16), S(DD))
+        w = wrap(16, 0, 0, "B2", "B3", R("EX"))
+        for h in range(2):
+            mm(R("B1", 128 * h, 128 * h + 128), R("EX", 128 * h, 128 * h + 128), R("IDF"), True, True)
+        tc(R("LST", 32, 48), w)
+        tc(R("MD"), I("ML", 0, 1280, "LST", 32, 48))
+        tc(R("OFD"), R("MD"))
+        act(R("TD", 0, 2048), I("X", 0, NX, "OFD", 0, 128), F.Copy)
+        act(R("TD", 2048, 4096), I("X", 0, NX, "OFD", 128, 256), F.Copy)
+        ts(R("INDD"), R("MD"), 0.0, A.is_gt)
+        ts(R("ZI", 0, 256), R("B1", 0, 256), R("LMF", 0, 1), A.mult)
+        ts(R("ZI", 0, 256), R("ZI", 0, 256), 1024, A.bitwise_and)
+        ts(R("CF", 0, 256), R("ZI", 0, 256), 1 / 32, A.mult, -16.0, A.add)
+        ts(R("CF", 256, 512), R("ZI", 0, 256), R("LMF", 5, 6), A.mult, R("LMF", 6, 7), A.add)
+        ts(R("CF", 512, 768), R("ZI", 0, 256), R("LMF", 3, 4), A.mult, R("LMF", 4, 5), A.add)
+
+        def firsts(i, b):
+            if i < 2:
+                h, gs, wd, rw = 0, range(4 * i, 4 * i + 4), 128, "RW1"
+            else:
+                h, gs, wd, rw = 1, range(2 * (i - 2), 2 * (i - 2) + 2), 256, "RW2"
+            for j, gg in enumerate(gs):
+                p0 = 32 * (gg // 2)
+                o = R(b, wd * j, wd * j + wd)
+                if j and p0 != 32 * (gs[j - 1] // 2):
+                    queue["p"].wait_ge(T.sem["p"], count["p"])
+                    known["p"]["p"] = count["p"]
+                mm(o, R("ONEB", 0, 128, 1, p0, p0 + 1), R("ROW", 512, 512 + wd, 1, p0, p0 + 1), True, False)
+                c = 256 + 256 * (gg % 2) + 128 * h
+                mm(o, R("CF", c, c + 128, 1, p0, p0 + 32), R("CF", 0, wd, 1, p0, p0 + 32), False, True)
+            return gs, wd, rw, h
+
+        def firsts2(i, b, r):
+            gs, wd, rw, h = r
+            scan(R("FS"), R(rw), R(b), A.mult, A.max)
+            tc(R("SM", 16 * FM + 8 * h + gs[0], 16 * FM + 8 * h + gs[0] + len(gs)), R("FS", wd - 1, 512, wd))
+        rr = [firsts(i, ("B3", "B5", "B6")[i]) for i in range(3)]
+        for k in range(4, 16):
+            tt(R("PR", 256 * k, 256 * k + 256), R("TX", k, 4096, 16), R("B4", 0, 256), A.mult)
+        for i in range(3):
+            firsts2(i, ("B3", "B5", "B6")[i], rr[i])
+        rr = [firsts(i + 3, ("B3", "B5", "B7")[i]) for i in range(3)]
+        for h in range(2):
+            o = R("B6", 256 * h, 256 * h + 256)
+            box = (T.BOX[:, :, :], [("BOX", 0, 256, 1)])
+            mm(o, R("PS", 128 * h, 128 * h + 128), box, True, False)
+            mm(o, R("PS", 256 + 128 * h, 384 + 128 * h), box, False, False)
+            mm(o, lone, row(768, 256), False, False)
+            for k in range(16):
+                for f, gw in ((0, "G2"), (16, "GM2")):
+                    mm(R("B6", 256 * h + f + k, 256 * h + 256, 32), R("PR", 256 * k + 128 * h, 256 * k + 128 * h + 128), R(gw), False, k == 15 and f == 16)
+        for i in range(3):
+            firsts2(i + 3, ("B3", "B5", "B7")[i], rr[i])
+        for b in range(8):
+            mm(R("B2", 8 * b, 8 * b + 8), R("IND", 128 * b, 128 * b + 128), R("GS0"), True, True)
+        tc(R("OCB"), R("B2", 0, 64))
+        mm(R("B2", 128, 192), R("TRJ"), R("OCB"), True, False)
+        for j in range(1, 8):
+            mm(R("B2", 128 + 8 * j, 192), R("ONEB"), R("OCB", 0, 64 - 8 * j), False, j == 7)
+        for h in range(2):
+            for j in range(8):
+                mm(R("B2", 192 + 8 * h, 200 + 8 * h), R("ONEB"), R("OCB", 8 * j, 8 * j + 8), j == 0, j == 7)
+        ts(S(NV), R("B2", 192, 208), -1.0, A.mult, 1024.0, A.add)
+        u, y = R("SM", 512, 576), R("SM", 576, 640)
+        tt(u, R("CI"), R("B2", 128, 192), A.subtract)
+        tt(y, R("B2", 128, 192), u, A.subtract)
+        ts(y, y, 1024.0, A.add)
+        tt(y, y, R("OCB"), A.mult)
+        tt(R("E1", 0, 1024, 16), y, u, A.add)
+        scan(R("B3", 0, 512), R("RM", 0, 512), R("E1", 0, 512), A.mult, A.add)
+        scan(R("B5", 0, 512), R("RM", 0, 512), R("E1", 512, 1024), A.mult, A.add)
+        tt(R("EM", 0, 512), R("B3"), R("QM", 0, 512), A.mult)
+        tt(R("EM", 512, 1024), R("B5"), R("QM", 0, 512), A.mult)
+        for b in range(8):
+            mm(R("B2", 256 + 8 * b, 264 + 8 * b), R("EM", 128 * b, 128 * b + 128), R("RB"), True, True)
+        tc(R("LST", 64, 128), R("B2", 256, 320))
+        tc(I("TB", 0, NE, "LST", 64, 128), R("TB", NE, NE + 1024))
+        scan(R("UD"), R("RM"), R("TD"), A.mult, A.max)
+        for h in range(2):
+            for k in range(16):
+                mm(R("B0", 128 * h + k, 128 * h + 128, 16), R("TD", 2048 * h + k, 2048 * h + 2048, 16), g8, True, True)
+            mm(R("B1", 8 * h, 8 * h + 8), R("INDD", 128 * h, 128 * h + 128), g8, True, True)
+        act(R("KA"), R("B0", 0, 256), F.Abs)
+        tt(R("VM"), R("US", 15, 4096, 16), R("UD", 15, 4096, 16), A.max)
+        for h in range(2):
+            mm(R("B1", 16 + 8 * h, 24 + 8 * h), R("VM", 128 * h, 128 * h + 128), g8, True, True)
+        scan(R("MSD"), R("BM"), R("KA"), A.max, A.min)
+        tt(S(FM), S(FM), C(2), A.is_equal)
+        tt(S(FM), S(FM), S(HAS), A.mult)
+        tt(S(T1), R("B1", 0, 16), S(NN), A.add)
+        ts(S(T1), S(T1), 16.0, A.is_le)
+        tt(S(FM), S(FM), S(T1), A.mult)
+        tt(S(MS), R("SI", 32, 48), R("MSD", 15, 256, 16), A.min)
+        tt(S(T2), R("B1", 16, 32), S(MS), A.subtract)
+        tt(S(T2), S(T2), R("LIM", 32, 48), A.is_le)
+        mer = R("SB", 0, 16)
+        tt(mer, S(FM), S(T2), A.mult)
+        tt(S(GR), S(SUU), R("SI", 32, 48), A.subtract)
+        tt(S(GR), S(GR), R("LIM", 16, 32), A.is_gt)
+        ts(S(NM), mer, -1.0, A.mult, 1.0, A.add)
+        tt(S(NM), S(NM), S(LIVE), A.mult)
+        want = R("SB", 16, 32)
+        tt(want, S(GR), S(NM), A.mult)
+
+        def ranks(bank, s):
+            mm(R(bank, 0, 8), R("TRI"), R("SB", s, s + 8), True, True)
+            mm(R(bank, 8, 16), R("TRI"), R("SB", s + 8, s + 16), True, False)
+            mm(R(bank, 8, 16), R("ONEB"), R("SB", s, s + 8), False, True)
+        ranks("B1", 16)
+        mm(R("B1", 32, 48), R("ONEB"), mer, True, True)
+        ts(S(T1), S(DD), float(NE), A.add)
+        tt(S(T1), S(T1), C(3), A.subtract)
+        tt(S(T1), S(T1), mer, A.mult)
+        tt(S(T2), S(DD), C(6 + t), A.subtract)
+        tt(S(T2), S(T2), mer, A.mult)
+        tt(R("E1", 512, 768, 16), S(T2), C(6 + t), A.add)
+        tc(S(RK), R("B1", 0, 16))
+        tt(S(SPL), S(RK), S(NV), A.is_lt)
+        tt(S(SPL), S(SPL), want, A.mult)
+        tt(R("SB", 32, 48), S(NM), S(SPL), A.subtract)
+        ranks("B0", 32)
+        tt(S(T2), S(RK), C(3), A.subtract)
+        tt(S(T2), S(T2), S(SPL), A.mult)
+        tt(S(T1), S(T1), S(T2), A.add)
+        tt(R("E1", 0, 256, 16), S(T1), C(3), A.add)
+        tt(S(T2), S(RK), C(10 + t), A.subtract)
+        tt(S(T2), S(T2), S(SPL), A.mult)
+        tt(R("E1", 256, 512, 16), S(T2), C(10 + t), A.add)
+        ts(S(VIS), R("B0", 0, 16), 64.0, A.is_lt)
+        tt(S(VIS), S(VIS), R("SB", 32, 48), A.mult)
+        tt(S(T2), R("B0", 0, 16), C(4), A.subtract)
+        tt(S(T2), S(T2), S(VIS), A.mult)
+        tt(R("E1", 768, 1024, 16), S(T2), C(4), A.add)
+        scan(R("B3"), R("RM", 0, 512), R("E1", 0, 512), A.mult, A.add)
+        scan(R("B5"), R("RM", 0, 512), R("E1", 512, 1024), A.mult, A.add)
+        tt(R("EM", 512, 1024), R("B5"), R("QM", 0, 512), A.mult)
+        tt(R("EM", 0, 512), R("B3"), R("QM", 0, 512), A.mult)
+        for b in (6, 7, 4, 5, 0, 1, 2, 3):
+            mm(R("B2", 8 * b, 8 * b + 8), R("EM", 128 * b, 128 * b + 128), R("RB"), True, True)
+        tc(R("LST", 128, 192), R("B2", 0, 64))
+        dst = (rank + 1 + t % (n - 1)) % n
+        src = (rank - 1 - t % (n - 1)) % n
+        tc(I("VS", 0, 336, "LST", 176, 192), xs)
+        send(dst, "XV%d" % t, 64, "VS", "va%d" % t, "vl%d" % t)
+        tc(R("MD"), I("ML", 0, 1280, "LST", 160, 176))
+        for h in range(2):
+            o = R("B7", 256 * h, 256 * h + 256)
+            mm(o, own(h), (T.IXA[:, :, :], [("IXA", 0, 256, 1)]), True, False)
+            mm(o, R("MD", 128 * h, 128 * h + 128), (T.IXB[:, :, :], [("IXB", 0, 256, 1)]), False, True)
+        ts(R("E2", 0, 512, 32), S(SPL), -1.0, A.add, BIG, A.mult)
+        ts(S(T1), mer, -2.0, A.mult, 1.0, A.add)
+        tt(S(T1), S(T1), S(SPL), A.subtract)
+        ts(R("E2", 16, 512, 32), S(T1), BIG, A.mult)
+        scan(R("TH"), R("RM", 0, 512), R("E2"), A.mult, A.add)
+        tt(R("PRS"), R("B6"), R("TH"), A.is_ge)
+        ts(R("TH"), R("PRS"), -1.0, A.mult, 1.0, A.add)
+        ts(S(AA), S(NN), -1.0, A.mult, 16.0, A.add)
+        tt(S(AA), S(AA), mer, A.mult)
+        tt(R("TH", 16, 512, 32), R("TH", 16, 512, 32), S(AA), A.add)
+        scan(R("B3"), R("RM", 0, 512), R("TH"), A.mult, A.add)
+        ts(R("ZI"), R("B3"), 4369.0, A.mult)
+        ts(R("ZI"), R("ZI"), 4680, A.bitwise_and)
+        tt(R("B5"), R("ZI"), R("B7"), A.add)
+        tt(w2(), R("B5"), R("PRS"), A.mult)
+        tc((T.F2[:, :, :], [("F2", 0, 256, 1)]), R3("W", 0, 16, 16, 32))
+        for h in range(2):
+            mm(R("B0", 128 * h, 128 * h + 128), R3("F2", 8 * h, 8 * h + 8, 0, 16), R("IDK"), True, True)
+        tc(R("NWE", 0, 4096, 16), I("TB", 0, NE + 1280, "LST", 144, 160))
+        tc(R("TG"), I("TB", 0, NE + 1280, "LST", 128, 144))
+        for q in range(16):
+            mm(R("B4", 0, 16), R("WQ", 128 * q, 128 * q + 128), R("TG", q, 256, 16), q == 0, q == 15)
+        tc(R("SI", 0, 256), R("B0", 0, 256))
+        ts(R("SI", 0, 256), R("SI", 0, 256), 8191, A.bitwise_and)
+        moved(R("SI", 0, 256), "MVO")
+        scan(R("VAL"), R("RM"), R("NWE"), A.mult, A.add)
+        act(I("OW", 0, NO, "MVO", 0, 256), R("VAL"), F.Silu)
+        tc(R("LST", 48, 64), R("B4", 0, 16))
+        for th, s in ((4096.0, 1), (512.0, 2), (64.0, 4)):
+            ts(R("B3"), w2(), -th, A.add, 0.0, A.max)
+            ts(R("B5"), w2(), -th, A.mult, th * th, A.add)
+            tt(R("TH"), w2(), R("B5"), A.min)
+            ts(R3("W", 15, 16, 24, 32), R("TH", 504, 512), 0.0, A.max)
+            tt((T.W[:, 0:15, :], [("W", 0, 480, 1)]), R("TH", 0, 480), R("B3", s, 480 + s), A.max)
+            tt(R3("W", 15, 16, 0, 32 - s), R("TH", 480, 512 - s), R("B3", 480 + s, 512), A.max)
+        h3 = lambda a, b: R3("H3", 0, 16, a, b)
+        ts(h3(0, 32), w2(), -8.0, A.add, 0.0, A.max)
+        ts(R("B5"), w2(), -8.0, A.mult, 64.0, A.add)
+        tt(w2(), w2(), R("B5"), A.min)
+        tt(R3("F1", 0, 16, 0, 16), R3("W", 0, 16, 0, 16), h3(8, 24), A.max)
+        tt(R3("F2", 0, 16, 0, 8), R3("W", 0, 16, 16, 24), h3(24, 32), A.max)
+        ts(R3("F2", 0, 16, 8, 16), R3("W", 0, 16, 24, 32), 0.0, A.max)
+        for j, f in ((0, "F1"), (256, "F2")):
+            for h in range(2):
+                mm(R("B7", j + 128 * h, j + 128 * h + 128), R3(f, 8 * h, 8 * h + 8, 0, 16), R("IDK"), True, True)
+        tc(R("ML", cl, 1024, 4), R("B7", 0, 256))
+        tc(R("L2"), R("B7", 256, 512))
+        tc(I("ML", 0, 1280, "LST", 48, 64), R("L2"))
+        if t < 3:
+            op("v", lambda: g.vector.tensor_reduce(T.SM[:, 400:401], T.B1[:, 32:48], AX, A.add), R("SM", 400, 401), [R("B1", 32, 48)])
+            tc(R("SI", 240, 241), R("SM", 400, 401))
+            ts(R("SI", 240, 241), R("SI", 240, 241), 15, A.bitwise_and)
+            tc(R("SM", 400, 401), R("SI", 240, 241))
+            ts(R("LIM", 32, 48), R("LIM", 0, 16), R("SM", 400, 401), A.add)
+        xv = "XV%d" % t
+        arrive("va%d" % t, xv)
+        for q in range(16):
+            mm(R("B2", 64, 68), R("WT", 128 * q, 128 * q + 128), R(xv, q, 64, 16), q == 0, q == 15)
+        tc(R("SI", 0, 4), R("B2", 64, 68))
+        ts(R("SI", 0, 4), R("SI", 0, 4), 4095, A.bitwise_and)
+        ts(R("LST", 192, 196), R("SI", 0, 4), 1, A.add)
+        tc(R("OVG"), I("OW", 0, NO, "LST", 192, 196))
+        tc(R("XVS", 0, 1024, 16), R(xv))
+        scan(R("XVE"), R("RM", 0, 1024), R("XVS"), A.mult, A.add)
+        for q in range(16):
+            mm(R("B2", 64, 68), R("WQ", 128 * q, 128 * q + 128), R("OVG", q, 64, 16), q == 0, q == 15)
+        tc(R("LST", 200, 204), R("B2", 64, 68))
+        tc(R("HL"), I("ML", 0, 1280, "LST", 200, 204))
+        tt(R("VD"), I("X", 0, NX, "HL", 0, 64), R("XVE"), A.subtract)
+        act(R("SQV"), R("VD"), F.Square)
+        mm(R("B0", 0, 128, 1, 0, 64), R("ONEB", 0, 64, 1, 0, 1), row(128, 128), True, False)
+        for k in range(16):
+            mm(R("B0", k, 128, 16, 0, 64), R("SQV", k, 1024, 16), R("G16"), False, k == 15)
+        scan(R("KB", 0, 128, 1, 0, 64), R("BM", 0, 128, 1, 0, 64), R("B0", 0, 128, 1, 0, 64), A.max, A.min)
+        tc(R("SI", 0, 8, 1, 0, 64), R("KB", 15, 128, 16, 0, 64))
+        ts(R("SI", 0, 8, 1, 0, 64), R("SI", 0, 8, 1, 0, 64), 15, A.bitwise_and)
+        tt(R("E1", 0, 128, 16, 0, 64), R("SI", 0, 8, 1, 0, 64), R("CO", 80, 88, 1, 0, 64), A.add)
+        scan(R("B3", 0, 128, 1, 0, 64), R("RM", 0, 128, 1, 0, 64), R("E1", 0, 128, 1, 0, 64), A.mult, A.add)
+        tt(R("EM", 0, 128, 1, 0, 64), R("B3", 0, 128, 1, 0, 64), R("QM", 0, 128, 1, 0, 64), A.mult)
+        mm(R("B2", 64, 68), R("EM", 0, 128, 1, 0, 64), R("RB", 0, 4, 1, 0, 64), True, True)
+        tc(R("LST", 208, 212), R("B2", 64, 68))
+        tc(R("SI", 64, 128), I("VD", 0, 1024, "LST", 208, 212))
+        ts(R("SI", 64, 128), R("SI", 64, 128), 1, A.arith_shift_right)
+        tc(R("RET"), R("SI", 64, 128))
+        send(src, "ME%d" % t, 64, "RET", "ra%d" % t, "rl%d" % t)
+        arrive("ra%d" % t, "ME%d" % t)
+        tt(R("NX1"), I("ME%d" % t, 0, 336, "LST", 176, 192), xs, A.add)
+        tc(I("X", 0, NX, "LST", 0, 16), R("NX1"))
+    dma("y", "ox", T.yx[:, :], T.X[:, 1:4097], R("X", 1, 4097)[1], [])
+    ts(R("VAL", 0, 1024), R("ML", 0, 1024), 0.0, A.is_equal, 4097.0, A.mult)
+    tt(R("VAL", 0, 1024), R("VAL", 0, 1024), R("ML", 0, 1024), A.add)
+    ts(R("VAL", 0, 1024), R("VAL", 0, 1024), -1.0, A.add)
+    dma("y", "oy", T.ym[:, :], T.VAL[:, 0:1024], R("VAL", 0, 1024)[1], [])
+    for k in ("dm", "dx", "da", "dl", "dw", "ox", "oy"):
+        g.sync.wait_ge(T.sem[k], count[k])
+    for k in ("v", "s", "p", "gg"):
+        g.sync.wait_ge(T.sem[k], count[k])
+    for t in range(4):
+        for k in ("vl", "rl"):
+            g.wait_ge(T.sem["%s%d" % (k, t)], count["%s%d" % (k, t)])

@@ -7,56 +7,34 @@ NE = 2064
 D0 = 4352
 BIG = float(2 ** 20)
 
-SCRATCH = {
-    "X": ("sbuf", [128, NX], "bfloat16"), "OW": ("sbuf", [128, NO], "float32"), "AC": ("sbuf", [128, NX], "int32"),
-    "ML": ("sbuf", [128, 1280], "float32"), "MI": ("sbuf", [128, 1280], "int32"), "TB": ("sbuf", [128, NE + 1280], "bfloat16"),
-    "TX": ("sbuf", [128, 4096], "bfloat16"), "US": ("sbuf", [128, 4096], "bfloat16"), "XE": ("sbuf", [128, 4096], "bfloat16"),
-    "XSE": ("sbuf", [128, 4096], "bfloat16"), "DF": ("sbuf", [128, 4096], "bfloat16"), "OWG": ("sbuf", [128, 4096], "bfloat16"),
-    "SQO": ("sbuf", [128, 4096], "bfloat16"), "SQ": ("sbuf", [128, 4096], "bfloat16"), "PR": ("sbuf", [128, 4096], "bfloat16"),
-    "TD": ("sbuf", [128, 4096], "bfloat16"), "UD": ("sbuf", [128, 4096], "bfloat16"), "VAL": ("sbuf", [128, 4096], "float32"),
-    "NWE": ("sbuf", [128, 4096], "bfloat16"), "RM": ("sbuf", [128, 4096], "bfloat16"),
-    "XS": ("sbuf", [128, 256], "bfloat16"), "ONE": ("sbuf", [128, 128], "float32"), "ONEB": ("sbuf", [128, 128], "bfloat16"), "IDF": ("sbuf", [128, 128], "float32"),
-    "IDK": ("sbuf", [128, 128], "float32"), "IDB": ("sbuf", [128, 128], "bfloat16"), "NID": ("sbuf", [128, 128], "bfloat16"),
-    "IDV": ("sbuf", [128, 128], "bfloat16"), "BO": ("sbuf", [128, 128], "bfloat16"), "G16": ("sbuf", [128, 8], "bfloat16"),
-    "G64": ("sbuf", [128, 8], "bfloat16"), "G2": ("sbuf", [128, 8], "bfloat16"), "GM2": ("sbuf", [128, 8], "bfloat16"),
-    "GS0": ("sbuf", [128, 8], "bfloat16"), "GS0F": ("sbuf", [128, 8], "float32"), "GD": ("sbuf", [128, 8], "bfloat16"), "GC": ("sbuf", [128, 32], "bfloat16"),
-    "QM": ("sbuf", [128, 1024], "float32"), "QI": ("sbuf", [128, 1280], "int32"), "QJ": ("sbuf", [128, 1280], "int32"),
-    "RB": ("sbuf", [128, 8], "float32"), "BM": ("sbuf", [128, 256], "bfloat16"), "ROW": ("sbuf", [128, 1024], "bfloat16"),
-    "WQ": ("sbuf", [128, 2048], "bfloat16"), "WT": ("sbuf", [128, 2048], "bfloat16"), "BOX": ("sbuf", [128, 8, 32], "bfloat16"),
-    "IXA": ("sbuf", [128, 8, 32], "float32"), "IXB": ("sbuf", [128, 8, 32], "float32"), "TRI": ("sbuf", [128, 128], "bfloat16"),
-    "TRJ": ("sbuf", [128, 128], "bfloat16"), "DUM": ("sbuf", [128, 256], "float32"), "CO": ("sbuf", [128, 256], "float32"),
-    "CI": ("sbuf", [128, 64], "float32"), "RW1": ("sbuf", [128, 512], "bfloat16"), "RW2": ("sbuf", [128, 512], "bfloat16"),
-    "LMI": ("sbuf", [128, 2], "int32"), "WTI": ("sbuf", [128, 1], "int32"), "LMF": ("sbuf", [128, 8], "float32"), "LIM": ("sbuf", [128, 64], "float32"),
-    "OFO": ("sbuf", [128, 256], "uint16"), "ACO": ("sbuf", [128, 256], "uint16"), "OFD": ("sbuf", [128, 256], "uint16"),
-    "MVO": ("sbuf", [128, 256], "uint16"), "LST": ("sbuf", [128, 512], "uint16"), "HL": ("sbuf", [128, 64], "uint16"),
-    "IND": ("sbuf", [128, 1024], "bfloat16"), "INDD": ("sbuf", [128, 256], "bfloat16"),
-    "K1": ("sbuf", [128, 256], "float32"), "KM": ("sbuf", [128, 256], "float32"), "KB": ("sbuf", [128, 256], "float32"),
-    "KD": ("sbuf", [128, 256], "float32"), "KA": ("sbuf", [128, 256], "float32"), "MSD": ("sbuf", [128, 256], "float32"),
-    "E1": ("sbuf", [128, 1024], "float32"), "EM": ("sbuf", [128, 1024], "float32"), "EX": ("sbuf", [128, 256], "float32"),
-    "E2": ("sbuf", [128, 512], "float32"), "TH": ("sbuf", [128, 512], "float32"), "EQ": ("sbuf", [128, 256], "float32"), "DS": ("sbuf", [128, 256], "float32"),
-    "SM": ("sbuf", [128, 1024], "float32"), "SI": ("sbuf", [128, 256], "int32"), "SB": ("sbuf", [128, 64], "bfloat16"),
-    "OCB": ("sbuf", [128, 64], "bfloat16"), "CF": ("sbuf", [128, 768], "bfloat16"), "FS": ("sbuf", [128, 512], "float32"),
-    "XB": ("sbuf", [128, 256], "bfloat16"), "PS": ("sbuf", [128, 512], "bfloat16"), "VM": ("sbuf", [128, 256], "bfloat16"),
-    "MD": ("sbuf", [128, 256], "float32"), "TG": ("sbuf", [128, 256], "bfloat16"), "PRS": ("sbuf", [128, 512], "float32"),
-    "W": ("sbuf", [128, 16, 32], "float32"), "H3": ("sbuf", [128, 16, 32], "float32"), "ZI": ("sbuf", [128, 512], "int32"),
-    "F1": ("sbuf", [128, 16, 16], "float32"), "F2": ("sbuf", [128, 16, 16], "float32"), "L2": ("sbuf", [128, 256], "float32"),
-    "VS": ("sbuf", [128, 336], "bfloat16"), "XVE": ("sbuf", [128, 1024], "bfloat16"), "XVS": ("sbuf", [128, 1024], "bfloat16"),
-    "VD": ("sbuf", [128, 1024], "bfloat16"), "SQV": ("sbuf", [128, 1024], "bfloat16"), "OVG": ("sbuf", [128, 64], "bfloat16"),
-    "RET": ("sbuf", [128, 64], "bfloat16"), "NX1": ("sbuf", [128, 256], "bfloat16"),
-}
-WIDTH = {k: v[1][1] for k, v in SCRATCH.items()}
-SHARE = {"SQ": "DF", "PR": "XSE", "TD": "SQO", "UD": "OWG", "NWE": "XE", "XVS": "XE", "E2": "E1", "FS": "TH", "KA": "K1", "MSD": "KM",
-         "L2": "MD", "ZI": "QI", "SQV": "SQO", "QJ": "MI"}
-for _k in SHARE:
-    del SCRATCH[_k]
+
+def _sb(spec):
+    d = {}
+    for dtype, names in spec.items():
+        for x in names.split():
+            k, w = x.split(":")
+            d[k] = ("sbuf", [128] + [int(v) for v in w.split("x")], dtype)
+    return d
+
+
+SCRATCH = _sb({
+    "bfloat16": "X:4368 TB:3344 TX:4096 US:4096 XE:4096 SQO:4096 SQ:4096 XA:4096 OWG:4096 RM:4096 ONEB:128 IDB:128 NID:128 "
+                "IDV:128 BO:128 G16:8 G64:8 GM1:8 GS0:8 GC:64 BM:256 ROW:1792 WQ:2048 WT:2048 TRI:128 TRJ:128 RW1:512 RW2:512 "
+                "IND:1024 XS:256 SB:64 OCB:64 CF:768 XB:256 VM:256 TG:256 PRS:512 E2:512 THB:512 "
+                "VS:336 XVE:1024 XVS:1024 VD:1024 OVG:64 RET:64",
+    "float32": "OW:8576 ML:1280 VAL:4096 ONE:128 IDF:128 IDK:128 GS0F:8 QM:1024 RB:8 IXA:8x32 IXB:8x32 DUM:256 CO:256 CI:64 "
+               "LMF:8 LIM:64 K1:256 KM:256 KB:256 KD:256 E1:1024 EM:1024 EX:256 EQ:256 DS:256 SM:1024 TH:512 MD:256 W:16x32 "
+               "H3:16x32 F1:16x16 F2:16x16",
+    "int32": "AC:4368 MI:1024 QI:1280 LMI:2 WTI:1 SI:256",
+    "uint16": "OFO:256 ACO:256 OFD:256 MVO:256 LST:512 HL:64"})
 for _t in range(4):
-    WIDTH["XV%d" % _t] = 64
-    WIDTH["ME%d" % _t] = 336
     SCRATCH["XV%d" % _t] = ("sbuf", [128, 64], "bfloat16")
     SCRATCH["ME%d" % _t] = ("sbuf", [128, 336], "bfloat16")
 for _b in range(8):
-    WIDTH["B%d" % _b] = 512
     SCRATCH["B%d" % _b] = ("psum", [128, 512], "float32")
+SHARE = {"SQB": "SQ", "XSE": "SQ", "THC": "CF", "NX1": "VM", "INDD": "TG", "TD": "XA", "UD": "OWG", "FS": "TH", "KA": "K1", "MSD": "KM", "L2": "MD", "ZI": "QI", "SQV": "XVE"}
+WIDTH = {k: v[1][1] for k, v in SCRATCH.items()}
+WIDTH.update({"SQB": 4096, "XSE": 4096, "THC": 512, "NX1": 256, "INDD": 256, "TD": 4096, "UD": 4096, "FS": 512, "KA": 256, "MSD": 256, "L2": 256, "ZI": 512, "SQV": 1024})
 SEMAPHORES = ["v", "s", "p", "gg", "dx", "da", "dm", "dl", "dw", "oy", "ox"] + ["%s%d" % (a, b) for a in ("va", "vl", "ra", "rl") for b in range(4)]
 PSUM = ["B%d" % b for b in range(8)]
 SIZE = {"float32": 4, "int32": 4, "bfloat16": 2, "uint16": 2}
@@ -131,15 +109,14 @@ def rank_program(g, core, T, topo):
             l = log.setdefault(b, [])
             l[:] = [r for r in l if not (r[:4] == (lo, hi, st, False) and r[4] == e)]
             l.append((lo, hi, st, False, e, c, dma))
-        if len(log) and any(b in PSUM for (b, _a, _b, _c) in reads + writes):
-            for b in set(x[0] for x in reads + writes if x[0] in PSUM):
-                if len(log[b]) > 60:
-                    m = {}
-                    for r in log[b]:
-                        k = (r[4], r[3])
-                        o = m.get(k)
-                        m[k] = r if o is None else (min(o[0], r[0]), max(o[1], r[1]), 1, r[3], r[4], max(o[5], r[5]), r[6])
-                    log[b] = list(m.values())
+        for b in set(x[0] for x in reads + writes if x[0] in PSUM):
+            if len(log[b]) > 60:
+                m = {}
+                for r in log[b]:
+                    k = (r[4], r[3])
+                    o = m.get(k)
+                    m[k] = r if o is None else (min(o[0], r[0]), max(o[1], r[1]), 1, r[3], r[4], max(o[5], r[5]), r[6])
+                log[b] = list(m.values())
 
     def op(q, f, out, ins):
         rd = [x for i in ins if isinstance(i, tuple) for x in i[1]]
@@ -169,11 +146,14 @@ def rank_program(g, core, T, topo):
     def ms(o, c):
         op("v", lambda: g.vector.memset(o[0], c), o, [])
 
-    def scan(o, d0, d1, f0, f1, init=0.0):
-        op("v", lambda: g.vector.tensor_tensor_scan(o[0], d0[0], d1[0], init, f0, f1), o, [d0, d1])
+    def scan(o, d0, d1, f0, f1):
+        op("v", lambda: g.vector.tensor_tensor_scan(o[0], d0[0], d1[0], 0.0, f0, f1), o, [d0, d1])
 
-    def act(o, i, f, **kw):
-        op("s", lambda: g.scalar.activation(o[0], i[0], f, **kw), o, [i])
+    def addup(o, i):
+        op("v", lambda: g.vector.tensor_reduce(o[0], i[0], AX, A.add), o, [i])
+
+    def act(o, i, f):
+        op("s", lambda: g.scalar.activation(o[0], i[0], f), o, [i])
 
     def mm(o, l, r, a, z):
         op("p", lambda: g.tensor.matmul(o[0], l[0], r[0], a, z), o, [l, r])
@@ -181,19 +161,16 @@ def rank_program(g, core, T, topo):
     def aff(o, i, pat, cmp, fill, base, cm):
         op("gg", lambda: g.affine_select(o[0], i[0], pat, cmp, fill, base, cm), o, [i])
 
-    def iota(o, pat, base, cm, **kw):
-        op("gg", lambda: g.iota(o[0], pat, base, cm, **kw), o, [])
+    def iota(o, pat, base, cm):
+        fl = SCRATCH[o[1][0][0]][2] != "int32"
+        op("gg", lambda: g.iota(o[0], pat, base, cm, allow_small_or_imprecise_dtypes=fl), o, [])
 
-    def dma(q, sem, o_ap, i_ap, reads, writes):
-        need(q, reads, writes, True)
-        queue[q].dma_start(o_ap, i_ap).then_inc(T.sem[sem], 16)
-        done(q, sem, 16, reads, writes, True)
+    def dma(sem, o_ap, i_ap, reads, writes):
+        need("y", reads, writes, True)
+        g.sync.dma_start(o_ap, i_ap).then_inc(T.sem[sem], 16)
+        done("y", sem, 16, reads, writes, True)
 
-    def fin(q, sem):
-        if known[q].get(sem, 0) < count[sem]:
-            queue[q].wait_ge(T.sem[sem], count[sem])
-
-    def send(dst, ob, osz, ib, rs, ls):
+    def send(dst, ob, ib, rs, ls):
         eng = topo.engines(core, T.cores[dst])[:4]
         mask = sum(1 << e for e in eng)
         rid, pid, _se = topo.addr(T.cores[dst])
@@ -211,188 +188,232 @@ def rank_program(g, core, T, topo):
         aff(o, o, pat, A.is_ge, 0.0, base, cm)
         aff(o, o, [[-s, k] for s, k in pat], A.is_ge, 0.0, width - 1 - base, -cm)
 
-    ms(R("X", 0, 16), -16.0)
-    ms(R("X", 4096, NX), 0.0)
-    ms(R("AC", 0, 8), 0)
-    ms(R("AC", 4096, NX), 0)
-    mi = R("MI", 0, 1024)
-    dma("y", "dm", mi[0], T.ml[:, :], [], mi[1])
-    dma("y", "dx", T.X[:, 1:4097], T.x0[:, :], [], R("X", 1, 4097)[1])
-    for j in range(4):
-        dma("y", "da", T.AC[:, 1 + 1024 * j:1025 + 1024 * j], T.ac[:, :], [], R("AC", 1 + 1024 * j, 1025 + 1024 * j)[1])
-    for b in ("AC",):
-        log[b] = [r[:5] + (64,) + r[6:] if r[4] == "da" else r for r in log[b]]
-    dma("y", "dl", T.LMI[:], T.lims[:, :], [], R("LMI")[1])
-    dma("y", "dw", T.WTI[:], T.wt[:, :], [], R("WTI")[1])
-    one = R("ONE", 0, 128)
-    ms(R("ONE"), 1.0)
-    iota(R("QI", 0, 1024), [[0, 64], [-1, 16]], 1024, 1)
-    ms(R("VAL"), 1.0)
-    aff(R("IDF"), one, [[-1, 128]], A.is_equal, 0.0, 0, 1)
-    iota(R("DUM"), [[16, 256]], D0, 1, allow_small_or_imprecise_dtypes=True)
-    ms(R("ML", 1024, 1280), 0.0)
-    ts(R("ML", 0, 1024), mi, 4096, A.is_equal, -4097, A.mult)
-    tt(R("ML", 0, 1024), R("ML", 0, 1024), mi, A.add)
-    ts(R("ML", 0, 1024), R("ML", 0, 1024), 1, A.add)
-    iota(R("QJ"), [[1, 1280]], 0, 0)
-    ts(R("QI", 0, 1024), R("QI", 0, 1024), 15, A.bitwise_and)
-    ts(R("QM"), R("QI", 0, 1024), 0, A.is_equal)
     q_ = lambda k: R("QM", k, k + 1)
-
-    def tmp(o, w, pats, src=None):
-        t = R("VAL", o, o + w)
-        for p in pats:
-            bounded(t, *p)
-        return t
-    bo = tmp(0, 128, [([[-16, 8], [0, 16]], 0, 1, 16)])
-    tc(R("BO"), bo)
-    rb = tmp(128, 8, [([[-16, 8]], 0, 1, 16)])
-    tc(R("RB"), rb)
-    tri = tmp(256, 128, [([[1, 128]], -1, -1, 200)])
-    tc(R("TRI"), tri)
-    trj = tmp(384, 128, [([[1, 128]], 0, -1, 200)])
-    tc(R("TRJ"), trj)
-    sel = R("VAL", 2048, 4096)
-    aff(sel, sel, [[1, 16], [0, 8], [-1, 16]], A.is_equal, 0.0, 0, 0)
-    bounded(sel, [[0, 16], [-16, 8], [0, 16]], 0, 1, 16)
-    tc(R("ONEB"), one)
-    tc(R("IDB"), R("IDF"))
-    ts(R("NID"), R("IDF"), -1.0, A.mult)
-    ts(R("IDK"), R("IDF"), 1024.0, A.mult)
-    ts(R("IDV"), R("IDF"), float(2 ** 18), A.mult)
+    C = lambda a: R("CO", 16 * a, 16 * a + 16)
+    S = lambda a, w=16: R("SM", 16 * a, 16 * a + w)
     g8 = R("BO", 0, 128, 16)
-    for b, c in (("G16", 16.0), ("G64", 65536.0), ("G2", 2.0), ("GM2", -2.0)):
-        ts(R(b), g8, c, A.mult)
-    ts(R("GS0"), g8, q_(0), A.mult)
-    ts(R("GS0F"), g8, q_(0), A.mult)
-    wc = R("SM", 0, 1)
-    ts(wc, q_(0), 128.0, A.mult)
-    tt(wc, wc, q_(1), A.add)
-    ts(R("SM", 1, 2), q_(6), -129.0, A.mult)
-    tt(wc, wc, R("SM", 1, 2), A.add)
-    ts(R("GD"), g8, wc, A.mult)
-    for u in range(4):
-        tt(R("SM", 2, 3), q_(2 + u), q_(6), A.subtract)
-        ts(R("GC", 8 * u, 8 * u + 8), g8, R("SM", 2, 3), A.mult, float(2 ** 17), A.mult)
-    ts(R("WQ"), sel, wc, A.mult)
-    tc(R("SM", 3, 4), R("WTI"))
-    ts(R("WT"), sel, R("SM", 3, 4), A.mult)
-    ms(R("RM"), 1.0)
-    ms(R("RM", 0, 4096, 16), 0.0)
-    ms(R("BM"), 0.0)
-    ms(R("BM", 0, 256, 16), float(2 ** 25))
-    for b, s in (("RW1", 128), ("RW2", 256)):
-        ms(R(b), 1.0)
-        ms(R(b, 0, 512, s), 0.0)
-    iota(R("EM", 0, 128), [[0, 8], [4096, 16]], 0, 0, allow_small_or_imprecise_dtypes=True)
-    iota(R("EM", 128, 256), [[0, 8], [1, 16]], 0, 0, allow_small_or_imprecise_dtypes=True)
-    iota(R("EM", 256, 384), [[0, 8], [-1, 16]], 15, 0, allow_small_or_imprecise_dtypes=True)
-    iota(R("EM", 512, 768), [[-1, 256]], 0, 0, allow_small_or_imprecise_dtypes=True)
-    tc(R("ROW", 0, 384), R("EM", 0, 384))
-    ms(R("ROW", 384, 512), -1.0)
-    tc(R("ROW", 512, 768), R("EM", 512, 768))
     row = lambda a, w: R("ROW", a, a + w, 1, 0, 1)
     lone = R("ONEB", 0, 128, 1, 0, 1)
-    b3 = R("BO", 0, 128)
-    ts(R3("BOX", 0, 8, 0, 16), b3, -1.0, A.mult)
-    tc(R3("BOX", 0, 8, 16, 32), b3)
-    ms(R3("IXA", 0, 8, 16, 32), 0.0)
-    ms(R3("IXB", 0, 8, 0, 16), 0.0)
-    ts(R3("IXA", 0, 8, 0, 16), R("IDF"), 2.0 ** -10, A.mult)
-    ts(R3("IXB", 0, 8, 16, 32), R("IDF"), 2.0 ** -10, A.mult)
-    ms((T.W[:, :, :], [("W", 0, 512, 1)]), 0.0)
+    one = R("ONE")
     w2 = lambda: (T.W[:, :, :], [("W", 0, 512, 1)])
-    ms(R3("W", 0, 16, 16, 32), -1.0)
-    tc(R("ROW", 768, 1024), (T.W[:, 0:8, :], [("W", 0, 512, 1)]))
-    C = lambda a: R("CO", 16 * a, 16 * a + 16)
-    iota(C(0), [[128, 2], [0, 8]], 4097, 1, allow_small_or_imprecise_dtypes=True)
-    iota(C(1), [[2048, 2], [0, 8]], 15, 16, allow_small_or_imprecise_dtypes=True)
-    iota(C(2), [[-128, 2], [0, 8]], 4096, -1, allow_small_or_imprecise_dtypes=True)
-    iota(C(3), [[128, 2], [0, 8]], NE + 1024, 1, allow_small_or_imprecise_dtypes=True)
-    iota(C(4), [[128, 2], [0, 8]], 64, 1, allow_small_or_imprecise_dtypes=True)
-    iota(C(5), [[0, 16]], 0, 16, allow_small_or_imprecise_dtypes=True)
-    for t in range(4):
-        iota(C(6 + t), [[512, 2], [0, 8]], t, 4, allow_small_or_imprecise_dtypes=True)
-        iota(C(10 + t), [[512, 2], [0, 8]], t + NE, 4, allow_small_or_imprecise_dtypes=True)
-    iota(R("CI"), [[128, 8], [0, 8]], 0, 1, allow_small_or_imprecise_dtypes=True)
-    pl = R("TB", NE, NE + 1280)
-    t1, t2 = R("VAL", 0, 1280), R("QI")
-    ts(t2, R("QJ"), 7, A.logical_shift_right)
-    ts(t1, t2, q_(0), A.mult, 128.0, A.add)
-    ts(t2, R("QJ"), 127, A.bitwise_and)
-    ts(R("E1", 0, 1024), R("QI", 0, 1024), q_(1), A.mult)
-    ts(R("EM", 0, 256), R("QI", 1024, 1280), q_(1), A.mult)
-    tt(R("VAL", 0, 1024), R("VAL", 0, 1024), R("E1", 0, 1024), A.add)
-    tt(R("VAL", 1024, 1280), R("VAL", 1024, 1280), R("EM", 0, 256), A.add)
-    ts(t2, R("QJ"), 3, A.bitwise_and)
-    ms(R("SM", 4, 6), 0.0)
-    for u in range(4):
-        ts(R("SM", 6, 7), q_(2 + u), float(u), A.mult)
-        tt(R("SM", 4, 5), R("SM", 4, 5), R("SM", 6, 7), A.add)
-        tt(R("SM", 5, 6), R("SM", 5, 6), q_(2 + u), A.add)
-    ts(R("E1", 0, 1024), R("QI", 0, 1024), R("SM", 4, 5), A.is_equal, R("SM", 5, 6), A.mult)
-    ts(R("EM", 0, 256), R("QI", 1024, 1280), R("SM", 4, 5), A.is_equal, R("SM", 5, 6), A.mult)
-    tt(R("TB", NE, NE + 1024), R("VAL", 0, 1024), R("E1", 0, 1024), A.add)
-    tt(R("TB", NE + 1024, NE + 1280), R("VAL", 1024, 1280), R("EM", 0, 256), A.add)
-    ms(R("TB", 0, NE), 128.0)
-    for k in range(11):
-        ms(R("SM", 16 + k, 17 + k), float(2 ** (10 - k)))
-    ms(R("SM", 27, 32), 0.0)
-    tt(R("SM", 16, 32), R("SM", 16, 32), R("QM", 0, 16), A.mult)
-    op("v", lambda: g.vector.tensor_reduce(T.LMF[:, 0:1], T.SM[:, 16:32], AX, A.add), R("LMF", 0, 1), [R("SM", 16, 32)])
-    iota(R("SI", 0, 1), [[0, 1]], 0, 1)
-    ts(R("SI", 0, 1), R("SI", 0, 1), 16, A.bitwise_and)
-    ts(R("LMF", 1, 2), R("SI", 0, 1), 16.0, A.is_equal)
-    ts(R("LMF", 2, 3), R("LMF", 1, 2), -1.0, A.mult, 1.0, A.add)
-    ts(R("LMF", 3, 4), R("LMF", 1, 2), 1 / 32, A.mult)
-    ts(R("LMF", 4, 5), R("LMF", 1, 2), -16.0, A.mult)
-    ts(R("LMF", 5, 6), R("LMF", 2, 3), 1 / 32, A.mult)
-    ts(R("LMF", 6, 7), R("LMF", 2, 3), -16.0, A.mult)
-    tc(R("SM", 8, 10), R("LMI"))
-    for j in range(2):
-        ts(R("K1", 0, 128), one, R("SM", 8 + j, 9 + j), A.mult)
-        for h in range(2):
-            mm(R("B0", 16 * j + 8 * h, 16 * j + 8 * h + 8), R("K1", 0, 128), R("GS0F"), True, True)
-    tc(R("LIM", 0, 32), R("B0", 0, 32))
-    tc(R("LIM", 32, 48), R("LIM", 0, 16))
-    for b, v in (("XE", 0.0), ("NWE", 0.0), ("E1", 0.0), ("E2", 0.0), ("VS", 0.0), ("XVS", 0.0)):
-        ms(R(b), v)
-    for t in range(4):
-        ms(R("ME%d" % t, 64, 336), 0.0)
-    ms(R("OW", 0, 16), 128.0)
 
-    def wrap(cols, e0, lo, bank, ps, keep=None):
+    def wrap(cols, bank, ps, keep=None):
         w = 16 * cols
         x = keep if keep is not None else R(ps, 0, w)
-        scan(x, R("RM", 0, w), R("E1", e0, e0 + w), A.mult, A.add)
+        scan(x, R("RM", 0, w), R("E1", 0, w), A.mult, A.add)
         tt(R("EM", 0, w), x, R("QM", 0, w), A.mult)
         for h in range(cols // 8):
             mm(R(bank, 8 * h, 8 * h + 8), R("EM", 128 * h, 128 * h + 128), R("RB"), True, True)
         return R(bank, 0, cols)
 
+    def wide(bank, lo, order):
+        scan(R("B3"), R("RM", 0, 512), R("E1", 0, 512), A.mult, A.add)
+        scan(R("B7"), R("RM", 0, 512), R("E1", 512, 1024), A.mult, A.add)
+        tt(R("EM", 512, 1024), R("B7"), R("QM", 0, 512), A.mult)
+        tt(R("EM", 0, 512), R("B3"), R("QM", 0, 512), A.mult)
+        for b in order:
+            mm(R(bank, lo + 8 * b, lo + 8 * b + 8), R("EM", 128 * b, 128 * b + 128), R("RB"), True, True)
+        return R(bank, lo, lo + 64)
+
     def moved(ids, b):
-        ts(R("EQ"), ids, 0.0, A.is_equal)
-        tt(R("EQ"), R("EQ"), R("DUM"), A.mult)
+        ts(R("B1", 0, 256), ids, 0.0, A.is_equal)
+        tt(R("EQ"), R("B1", 0, 256), R("DUM"), A.mult)
         tt(R("EQ"), R("EQ"), ids, A.add)
         tc(R(b), R("EQ"))
 
     def owners(b):
-        moved(R("ML", 256 * b, 256 * b + 256), "MVO")
-        tc(R("NWE", 0, 4096, 16), R("TB", NE + 256 * b, NE + 256 * b + 256))
-        scan(R("VAL"), R("RM"), R("NWE"), A.mult, A.add)
-        act(I("OW", 0, NO, "MVO", 0, 256), R("VAL"), F.Silu)
+        mv = ("MVO", "OFD")[b % 2]
+        moved(R("ML", 256 * b, 256 * b + 256), mv)
+        tc(R("XE", 0, 4096, 16), R("TB", NE + 256 * b, NE + 256 * b + 256))
+        settle(mv)
 
-    S = lambda a, w=16: R("SM", 16 * a, 16 * a + w)
+    def settle(mv):
+        for h in range(2):
+            v = R("VAL", 2048 * h, 2048 * h + 2048)
+            scan(v, R("RM", 0, 2048), R("XE", 2048 * h, 2048 * h + 2048), A.mult, A.add)
+            act(I("OW", 0, NO, mv, 128 * h, 128 * h + 128), v, F.Silu)
+
+    mi = R("MI")
+    dma("dm", T.MI[:, :], T.ml[:, :], [], mi[1])
+    ms(R("X", 0, 16), -16.0)
+    ms(R("X", 4096, NX), 0.0)
+    ms(R("AC", 0, 8), 0)
+    ms(R("AC", 4096, NX), 0)
+    dma("dx", T.X[:, 1:4097], T.x0[:, :], [], R("X", 1, 4097)[1])
+    for j in range(4):
+        dma("da", T.AC[:, 1 + 1024 * j:1025 + 1024 * j], T.ac[:, :], [], R("AC", 1 + 1024 * j, 1025 + 1024 * j)[1])
+    log["AC"] = [r[:5] + (64,) + r[6:] if r[4] == "da" else r for r in log["AC"]]
+    dma("dl", T.LMI[:], T.lims[:, :], [], R("LMI")[1])
+    dma("dw", T.WTI[:], T.wt[:, :], [], R("WTI")[1])
+    iota(R("QI", 0, 1024), [[0, 64], [-1, 16]], 1024, 1)
+    iota(R("QI", 1024, 1280), [[1, 256]], 0, 0)
+    iota(R("DUM"), [[16, 256]], D0, 1)
+    ms(R("XE"), 0.0)
+    ms(R("RM"), 1.0)
+    ms(R("RM", 0, 4096, 16), 0.0)
+    ms(R("OW", 0, 16), 128.0)
+    ms(one, 1.0)
+    ts(R("QI", 0, 1024), R("QI", 0, 1024), 15, A.bitwise_and)
+    ts(R("QM"), R("QI", 0, 1024), 0, A.is_equal)
+    ms(R("SM", 4, 6), 0.0)
+    for u in range(4):
+        ts(R("SM", 6, 7), q_(2 + u), float(u), A.mult)
+        tt(R("SM", 4, 5), R("SM", 4, 5), R("SM", 6, 7), A.add)
+        tt(R("SM", 5, 6), R("SM", 5, 6), q_(2 + u), A.add)
+    ci, cj = R("QI", 1024, 1280), R("SI")
+    ts(cj, ci, 7, A.logical_shift_right)
+    ts(R("K1"), cj, q_(0), A.mult, 128.0, A.add)
+    ts(cj, ci, 127, A.bitwise_and)
+    ts(R("KM"), cj, q_(1), A.mult)
+    tt(R("K1"), R("K1"), R("KM"), A.add)
+    ts(cj, ci, 3, A.bitwise_and)
+    ts(R("KM"), cj, R("SM", 4, 5), A.is_equal, R("SM", 5, 6), A.mult)
+    tt(R("TB", NE, NE + 256), R("K1"), R("KM"), A.add)
+    ml = R("ML", 0, 1024)
+    ts(ml, mi, 4096, A.is_equal, -4097, A.mult)
+    tt(ml, ml, mi, A.add)
+    ts(ml, ml, 1, A.add)
+    owners(0)
+    for b in range(1, 5):
+        ts(R("SM", 7, 8), q_(0), 2.0 * b, A.mult)
+        ts(R("TB", NE + 256 * b, NE + 256 * b + 256), R("TB", NE, NE + 256), R("SM", 7, 8), A.add)
+    ms(R("ML", 1024, 1280), 0.0)
+    act(R("IND"), ml, F.Sign)
+    aff(R("IDF"), one, [[-1, 128]], A.is_equal, 0.0, 0, 1)
+    ms(R("TH"), 1.0)
+    for o, w, p in ((0, 128, ([[-16, 8], [0, 16]], 0, 1, 16)), (128, 8, ([[-16, 8]], 0, 1, 16)), (256, 128, ([[1, 128]], -1, -1, 200)),
+                    (384, 128, ([[1, 128]], 0, -1, 200))):
+        bounded(R("TH", o, o + w), *p)
+    tc(R("BO"), R("TH", 0, 128))
+    tc(R("RB"), R("TH", 128, 136))
+    tc(R("TRI"), R("TH", 256, 384))
+    tc(R("TRJ"), R("TH", 384, 512))
+    tc(R("ONEB"), one)
+    tc(R("IDB"), R("IDF"))
+    ts(R("NID"), R("IDF"), -1.0, A.mult)
+    ts(R("IDK"), R("IDF"), 1024.0, A.mult)
+    ts(R("IDV"), R("IDF"), float(2 ** 18), A.mult)
+    for b, c in (("G16", 16.0), ("G64", 65536.0), ("GM1", -1.0)):
+        ts(R(b), g8, c, A.mult)
+    ts(R("GS0"), g8, q_(0), A.mult)
+    ts(R("GS0F"), g8, q_(0), A.mult)
+    for o, pat, base in ((0, [[0, 8], [4096, 16]], 0), (128, [[0, 8], [1, 16]], 0), (256, [[0, 8], [-1, 16]], 15), (512, [[-1, 256]], 0)):
+        w = pat[0][1] * (pat[1][1] if len(pat) > 1 else 1)
+        iota(R("EM", o, o + w), pat, base, 0)
+    tc(R("ROW", 0, 384), R("EM", 0, 384))
+    ms(R("ROW", 384, 512), -1.0)
+    tc(R("ROW", 512, 768), R("EM", 512, 768))
+    ms(w2(), 0.0)
+    ms(R3("W", 0, 16, 16, 32), -1.0)
+    tc(R("ROW", 768, 1280), w2())
+    ms(R("ROW", 1280, 1792), 0.0)
+    for h in range(2):
+        tc(R("ROW", 1280 + 256 * h, 1408 + 256 * h), R("EM", 128, 256))
+    ms(R("BM"), 0.0)
+    ms(R("BM", 0, 256, 16), float(2 ** 25))
+    wc = R("SM", 0, 1)
+    ts(wc, q_(0), 128.0, A.mult)
+    tt(wc, wc, q_(1), A.add)
+    ts(R("SM", 1, 2), q_(6), -129.0, A.mult)
+    tt(wc, wc, R("SM", 1, 2), A.add)
+    for u in range(4):
+        tt(R("SM", 2, 3), q_(2 + u), q_(6), A.subtract)
+        ts(R("GC", 16 * u + 8, 16 * u + 16), g8, wc, A.mult)
+        ts(R("GC", 16 * u, 16 * u + 8), g8, R("SM", 2, 3), A.mult, float(2 ** 17), A.mult)
+    lanes = lambda a, base, s: iota(C(a), [[128 * s, 2], [0, 8]], base, s)
+    lanes(0, 4097, 1)
+    lanes(1, 15, 16)
+    lanes(2, 4096, -1)
+    lanes(3, NE + 1024, 1)
+    lanes(4, 64, 1)
+    iota(C(5), [[0, 16]], 0, 16)
+    for t in range(4):
+        lanes(6 + t, t, 4)
+        lanes(10 + t, t + NE, 4)
+    iota(R("CI"), [[128, 8], [0, 8]], 0, 1)
+    iota(R("SI", 0, 1), [[0, 1]], 0, 1)
+    ms(R("E1"), 0.0)
+    ms(R("WQ"), 1.0)
+    aff(R("WQ"), R("WQ"), [[1, 16], [0, 8], [-1, 16]], A.is_equal, 0.0, 0, 0)
+    bounded(R("WQ"), [[0, 16], [-16, 8], [0, 16]], 0, 1, 16)
+    owners(1)
+
+    def rest():
+        ms(R("TB", 0, NE), 128.0)
+        for b, s in (("RW1", 128), ("RW2", 256)):
+            ms(R(b), 1.0)
+            ms(R(b, 0, 512, s), 0.0)
+        ms(R3("IXA", 0, 8, 16, 32), 0.0)
+        ms(R3("IXB", 0, 8, 0, 16), 0.0)
+        ts(R3("IXA", 0, 8, 0, 16), R("IDF"), 2.0 ** -10, A.mult)
+        ts(R3("IXB", 0, 8, 16, 32), R("IDF"), 2.0 ** -10, A.mult)
+        for k in range(11):
+            ms(R("SM", 16 + k, 17 + k), float(2 ** (10 - k)))
+        ms(R("SM", 27, 32), 0.0)
+        tt(R("SM", 16, 32), R("SM", 16, 32), R("QM", 0, 16), A.mult)
+        addup(R("LMF", 0, 1), R("SM", 16, 32))
+        ts(R("LMF", 2, 3), R("LMF", 1, 2), -1.0, A.mult, 1.0, A.add)
+        for a in (0, 1):
+            ts(R("LMF", 3 + 2 * a, 4 + 2 * a), R("LMF", 1 + a, 2 + a), 1 / 32, A.mult)
+            ts(R("LMF", 4 + 2 * a, 5 + 2 * a), R("LMF", 1 + a, 2 + a), -16.0, A.mult)
+        tc(R("SM", 8, 10), R("LMI"))
+        for j in range(2):
+            ts(R("VM", 0, 128), one, R("SM", 8 + j, 9 + j), A.mult)
+            for h in range(2):
+                mm(R("B2", 16 * j + 8 * h, 16 * j + 8 * h + 8), R("VM", 0, 128), R("GS0"), True, True)
+        tc(R("LIM", 0, 32), R("B2", 0, 32))
+        tc(R("LIM", 32, 48), R("LIM", 0, 16))
+        for b in ("VS", "XVS", "E2"):
+            ms(R(b), 0.0)
+        for u in range(4):
+            ms(R("ME%d" % u, 64, 336), 0.0)
+        tc(R("SM", 3, 4), R("WTI"))
+        ts(R("WT"), R("WQ"), R("SM", 3, 4), A.mult)
+        ts(R("WQ"), R("WQ"), wc, A.mult)
+
+    ts(R("SI", 0, 1), R("SI", 0, 1), 16, A.bitwise_and)
+    ts(R("LMF", 1, 2), R("SI", 0, 1), 16.0, A.is_equal)
     NN, LIVE, HAS, FM, DD, MS, GR, WAN, SPL, RK, IDL, VIS, T1, T2, RV = range(4, 19)
     SUU, S1, NV, NM, AA = 20, 21, 22, 23, 24
+
+    def empties():
+        for b in range(8):
+            mm(R("B2", 64 + 8 * b, 72 + 8 * b), R("IND", 128 * b, 128 * b + 128), R("GS0"), True, True)
+        tc(R("OCB"), R("B2", 64, 128))
+        mm(R("B2", 128, 192), R("TRJ"), R("OCB"), True, False)
+        for j in range(1, 8):
+            mm(R("B2", 128 + 8 * j, 192), R("ONEB"), R("OCB", 0, 64 - 8 * j), False, j == 7)
+        for h in range(2):
+            for j in range(8):
+                mm(R("B2", 192 + 8 * h, 200 + 8 * h), R("ONEB"), R("OCB", 8 * j, 8 * j + 8), j == 0, j == 7)
+        u, y = R("SM", 512, 576), R("SM", 576, 640)
+        tt(u, R("CI"), R("B2", 128, 192), A.subtract)
+        ts(S(NV), R("B2", 192, 208), -1.0, A.mult, 1024.0, A.add)
+        tt(y, R("B2", 128, 192), u, A.subtract)
+        ts(y, y, 1024.0, A.add)
+        tt(y, y, R("OCB"), A.mult)
+        tt(R("E1", 0, 1024, 16), y, u, A.add)
+        tc(R("LST", 64, 128), wide("B2", 256, range(8)))
+        tc(I("TB", 0, NE, "LST", 64, 128), R("TB", NE, NE + 1024))
 
     for t in range(4):
         cl = t & 3
         own = lambda h, b="ML": R(b, cl + 512 * h, cl + 512 * h + 512, 4)
-        tc(R("OFO"), R("ML", cl, 1024, 4))
-        tc(R("TX", 0, 2048), I("X", 0, NX, "OFO", 0, 128))
-        act(R("TX", 2048, 4096), I("X", 0, NX, "OFO", 128, 256), F.Copy)
-        ts(R("IND"), R("ML", 0, 1024), 0.0, A.is_gt)
+        half = lambda b, h: R(b, 2048 * h, 2048 * h + 2048)
+
+        def squares(out, win, w, bank, kk):
+            for j in range(2):
+                o = R(bank, 256 * j, 256 * j + 256)
+                mm(o, R("IDB"), R(win, 2 * kk + j, 4096, 16), True, False)
+                mm(o, R("NID"), w, False, True)
+            act(R(out, 512 * kk, 512 * kk + 512), R(bank), F.Square)
+        if t == 0:
+            tc(R("OFO"), R("ML", 0, 1024, 4))
+        tc(half("TX", 0), I("X", 0, NX, "OFO", 0, 128))
+        if t == 0:
+            tc(half("TX", 1), I("X", 0, NX, "OFO", 128, 256))
+        else:
+            act(half("TX", 1), I("X", 0, NX, "OFO", 128, 256), F.Copy)
         for h in range(2):
             o = R("B0", 128 * h, 128 * h + 128)
             mm(o, own(h), R("IDF"), True, False)
@@ -402,77 +423,59 @@ def rank_program(g, core, T, topo):
                 mm(R("B0", 128 * h + k, 128 * h + 128, 16), R("TX", 2048 * h + k, 2048 * h + 2048, 16), R("G64"), False, k == 15)
         act(R("K1"), R("B0", 0, 256), F.Abs)
         for h in range(2):
-            mm(R("B1", 8 * h, 8 * h + 8), own(h, "IND"), g8, True, True)
-        scan(R("US", 0, 2048), R("RM", 0, 2048), R("TX", 0, 2048), A.mult, A.max)
-        scan(R("KM"), R("BM"), R("K1"), A.max, A.min)
-        tc(S(NN), R("B1", 0, 16))
+            mm(R("B2", 8 * h, 8 * h + 8), own(h, "IND"), g8, True, True)
+        scan(half("US", 0), half("RM", 0), half("TX", 0), A.mult, A.max)
+        tc(S(NN), R("B2", 0, 16))
         ts(S(LIVE), S(NN), 0.0, A.is_gt)
+        scan(R("KM"), R("BM"), R("K1"), A.max, A.min)
         tc(R("SI", 0, 16), R("KM", 15, 256, 16))
         ts(R("SI", 16, 32), R("SI", 0, 16), 4095, A.bitwise_and)
-        ts(R("SI", 32, 48), R("SI", 0, 16), 16, A.logical_shift_right)
         ts(S(T1), R("SI", 16, 32), 1.0, A.add)
         tt(S(T1), S(T1), C(0), A.subtract)
         tt(S(T1), S(T1), S(LIVE), A.mult)
         tt(R("E1", 0, 256, 16), S(T1), C(0), A.add)
-        w = wrap(16, 0, 0, "B2", "B3")
+        w = wrap(16, "B2", "B3")
         tc(R("LST", 0, 16), w)
-        tc(R("XE", 0, 4096, 16), I("X", 0, NX, "LST", 0, 16))
         ts(R("ACO"), I("AC", 0, NX, "LST", 0, 16), 1, A.add)
         xs = R("XS")
-        tc(xs, R("XE", 0, 4096, 16))
-        scan(R("XSE"), R("RM"), R("XE"), A.mult, A.add)
-        for kk in range(8):
-            b = ("B4", "B5", "B6")[kk % 3]
-            for j in range(2):
-                o = R(b, 256 * j, 256 * j + 256)
-                mm(o, R("IDB"), R("TX", 2 * kk + j, 4096, 16), True, False)
-                mm(o, R("NID"), xs, False, True)
-            act(R("SQO", 512 * kk, 512 * kk + 512), R(b), F.Square)
+        tc(xs, I("X", 0, NX, "LST", 0, 16))
         if t == 0:
-            for b in range(4):
-                owners(b)
+            owners(2)
+        tc(R("XE", 0, 4096, 16), xs)
+        scan(R("XSE"), R("RM"), R("XE"), A.mult, A.add)
+        if t == 0:
+            owners(3)
         for h in range(2):
-            act(R("OWG", 2048 * h, 2048 * h + 2048), I("OW", 0, NO, "ACO", 128 * h, 128 * h + 128), F.Copy)
-        scan(R("US", 2048, 4096), R("RM", 2048, 4096), R("TX", 2048, 4096), A.mult, A.max)
+            act(half("OWG", h), I("OW", 0, NO, "ACO", 128 * h, 128 * h + 128), F.Copy)
         for h in range(2):
-            mm(R("B1", 16 + 8 * h, 24 + 8 * h), R("US", 2048 * h + 15, 2048 * h + 2048, 16), g8, True, True)
+            tt(half("XA", h), I("X", 0, NX, "ACO", 128 * h, 128 * h + 128), half("XSE", h), A.subtract)
+            act(half("XA", h), half("XA", h), F.Square)
+        if t == 0:
+            rest()
+            empties()
+        ts(R("SI", 32, 48), R("SI", 0, 16), 16, A.logical_shift_right)
+        scan(half("US", 1), half("RM", 1), half("TX", 1), A.mult, A.max)
         for h in range(2):
-            o = R("B3", 128 * h, 128 * h + 128)
-            mm(o, own(h, "IND"), R("IDV"), True, False)
-            mm(o, lone, row(256, 128), False, False)
+            mm(R("B2", 16 + 8 * h, 24 + 8 * h), R("US", 2048 * h + 15, 2048 * h + 2048, 16), g8, True, True)
+        tc(S(SUU), R("B2", 16, 32))
+        mm(R("B0"), lone, row(1280, 512), True, False)
+        for h in range(2):
             for k in range(16):
-                mm(R("B3", 128 * h + k, 128 * h + 128, 16), R("SQO", 256 * k + 128 * h, 256 * k + 128 * h + 128), R("G16"), False, k == 15)
+                mm(R("B0", 256 * h + k, 256 * h + 256, 16), R("OWG", 2048 * h + k, 2048 * h + 2048, 16), R("GC", 16 * cl, 16 * cl + 16), False, False)
         for h in range(2):
-            tt(R("DF", 2048 * h, 2048 * h + 2048), I("X", 0, NX, "ACO", 128 * h, 128 * h + 128), R("XSE", 2048 * h, 2048 * h + 2048), A.subtract)
-            act(R("SQ", 2048 * h, 2048 * h + 2048), R("DF", 2048 * h, 2048 * h + 2048), F.Square)
-        tc(S(SUU), R("B1", 16, 32))
-        scan(R("KB"), R("RM", 0, 256), R("B3", 0, 256), A.mult, A.max)
-        tc(R("SI", 48, 64), R("KB", 15, 256, 16))
-        ts(R("SI", 48, 64), R("SI", 48, 64), 15, A.bitwise_and)
-        tt(R("E1", 0, 256, 16), C(1), R("SI", 48, 64), A.subtract)
-        w = wrap(16, 0, 0, "B2", "B3")
-        tc(R("LST", 16, 32), w)
-        tc(R("XB"), I("TX", 0, 4096, "LST", 16, 32))
-        mm(R("B4", 0, 256), R("IDB"), xs, True, False)
-        mm(R("B4", 0, 256), R("NID"), R("XB"), False, True)
+            for k in range(16):
+                mm(R("B0", 256 * h + k, 256 * h + 128, 16), R("XA", 2048 * h + k, 2048 * h + 2048, 16), R("G16"), False, h == 1 and k == 15)
+        for kk in range(5):
+            squares("SQO", "TX", xs, ("B4", "B5")[kk % 2], kk)
+        hv = lambda b, h: R(b, 128 * h, 128 * h + 128)
         for h in range(2):
-            o = R("B0", 128 * h, 128 * h + 128)
-            mm(o, lone, row(128, 128), True, False)
-            for k in range(16):
-                c = R("B0", 128 * h + k, 128 * h + 128, 16)
-                mm(c, R("OWG", 2048 * h + k, 2048 * h + 2048, 16), R("GC", 8 * cl, 8 * cl + 8), False, False)
-                mm(R("B5", 128 * h + k, 128 * h + 128, 16), R("OWG", 2048 * h + k, 2048 * h + 2048, 16), R("GD"), True, True)
-            for k in range(16):
-                mm(R("B0", 128 * h + k, 128 * h + 128, 16), R("SQ", 2048 * h + k, 2048 * h + 2048, 16), R("G16"), False, k == 15)
-        tt(R("PS", 0, 256), xs, R("B4", 0, 256), A.mult)
-        tt(R("PS", 256, 512), R("XB"), R("B4", 0, 256), A.mult)
-        for k in range(4):
-            tt(R("PR", 256 * k, 256 * k + 256), R("TX", k, 4096, 16), R("B4", 0, 256), A.mult)
-        scan(R("KD"), R("BM"), R("B0", 0, 256), A.max, A.min)
+            scan(hv("KD", h), R("BM", 0, 128), R("B0", 256 * h, 256 * h + 128), A.max, A.min)
         tc(R("E1", 0, 256, 16), R("KD", 15, 256, 16))
         scan(R("EX"), R("RM", 0, 256), R("E1", 0, 256), A.mult, A.add)
-        tt(R("EQ"), R("EX"), R("B0", 0, 256), A.is_equal)
-        tt(R("EQ"), R("EQ"), R("B5", 0, 256), A.mult)
+        for h in range(2):
+            tt(hv("EQ", h), hv("EX", h), R("B0", 256 * h, 256 * h + 128), A.is_equal)
+        for h in range(2):
+            tt(hv("EQ", h), hv("EQ", h), R("B0", 256 * h + 128, 256 * h + 256), A.mult)
         scan(R("DS"), R("RM", 0, 256), R("EQ"), A.mult, A.add)
         ts(S(HAS), R("KD", 15, 256, 16), float(2 ** 17), A.is_lt)
         tt(S(HAS), S(HAS), S(LIVE), A.mult)
@@ -480,20 +483,37 @@ def rank_program(g, core, T, topo):
         tt(S(T1), S(T1), S(HAS), A.mult)
         ts(S(DD), S(T1), float(cl), A.add)
         tc(R("E1", 0, 256, 16), S(DD))
-        w = wrap(16, 0, 0, "B2", "B3", R("EX"))
+        w = wrap(16, "B2", "B3", R("EX"))
         for h in range(2):
             mm(R("B1", 128 * h, 128 * h + 128), R("EX", 128 * h, 128 * h + 128), R("IDF"), True, True)
+        for kk in range(5, 8):
+            squares("SQO", "TX", xs, ("B4", "B5")[kk % 2], kk)
         tc(R("LST", 32, 48), w)
         tc(R("MD"), I("ML", 0, 1280, "LST", 32, 48))
         tc(R("OFD"), R("MD"))
-        act(R("TD", 0, 2048), I("X", 0, NX, "OFD", 0, 128), F.Copy)
-        act(R("TD", 2048, 4096), I("X", 0, NX, "OFD", 128, 256), F.Copy)
-        ts(R("INDD"), R("MD"), 0.0, A.is_gt)
+        for h in range(2):
+            act(half("TD", h), I("X", 0, NX, "OFD", 128 * h, 128 * h + 128), F.Copy)
+        act(R("INDD"), R("MD"), F.Sign)
         ts(R("ZI", 0, 256), R("B1", 0, 256), R("LMF", 0, 1), A.mult)
         ts(R("ZI", 0, 256), R("ZI", 0, 256), 1024, A.bitwise_and)
         ts(R("CF", 0, 256), R("ZI", 0, 256), 1 / 32, A.mult, -16.0, A.add)
         ts(R("CF", 256, 512), R("ZI", 0, 256), R("LMF", 5, 6), A.mult, R("LMF", 6, 7), A.add)
         ts(R("CF", 512, 768), R("ZI", 0, 256), R("LMF", 3, 4), A.mult, R("LMF", 4, 5), A.add)
+        for h in range(2):
+            o = R("B0", 128 * h, 128 * h + 128)
+            mm(o, own(h, "IND"), R("IDV"), True, False)
+            mm(o, lone, row(256, 128), False, False)
+            for k in range(16):
+                mm(R("B0", 128 * h + k, 128 * h + 128, 16), R("SQO", 256 * k + 128 * h, 256 * k + 128 * h + 128), R("G16"), False, k == 15)
+
+        def leave(h, sq, signs, stop):
+            for k in range(16):
+                for f in range(2):
+                    mm(R("B6", 256 * h + 16 * f + k, 256 * h + 256, 32), R(sq, 256 * k + 128 * h, 256 * k + 128 * h + 128), signs[f], False,
+                       stop and h == 1 and k == 15 and f == 1)
+        mm(R("B6"), lone, row(768, 512), True, False)
+        for h in range(2):
+            leave(h, "SQO", (R("GM1"), g8), False)
 
         def firsts(i, b):
             if i < 2:
@@ -509,75 +529,57 @@ def rank_program(g, core, T, topo):
                 mm(o, R("ONEB", 0, 128, 1, p0, p0 + 1), R("ROW", 512, 512 + wd, 1, p0, p0 + 1), True, False)
                 c = 256 + 256 * (gg % 2) + 128 * h
                 mm(o, R("CF", c, c + 128, 1, p0, p0 + 32), R("CF", 0, wd, 1, p0, p0 + 32), False, True)
-            return gs, wd, rw, h
+            return gs, wd, rw, h, b
 
-        def firsts2(i, b, r):
-            gs, wd, rw, h = r
+        def firsts2(r):
+            gs, wd, rw, h, b = r
             scan(R("FS"), R(rw), R(b), A.mult, A.max)
             tc(R("SM", 16 * FM + 8 * h + gs[0], 16 * FM + 8 * h + gs[0] + len(gs)), R("FS", wd - 1, 512, wd))
-        rr = [firsts(i, ("B3", "B5", "B6")[i]) for i in range(3)]
-        for k in range(4, 16):
-            tt(R("PR", 256 * k, 256 * k + 256), R("TX", k, 4096, 16), R("B4", 0, 256), A.mult)
-        for i in range(3):
-            firsts2(i, ("B3", "B5", "B6")[i], rr[i])
-        rr = [firsts(i + 3, ("B3", "B5", "B7")[i]) for i in range(3)]
-        for h in range(2):
-            o = R("B6", 256 * h, 256 * h + 256)
-            box = (T.BOX[:, :, :], [("BOX", 0, 256, 1)])
-            mm(o, R("PS", 128 * h, 128 * h + 128), box, True, False)
-            mm(o, R("PS", 256 + 128 * h, 384 + 128 * h), box, False, False)
-            mm(o, lone, row(768, 256), False, False)
-            for k in range(16):
-                for f, gw in ((0, "G2"), (16, "GM2")):
-                    mm(R("B6", 256 * h + f + k, 256 * h + 256, 32), R("PR", 256 * k + 128 * h, 256 * k + 128 * h + 128), R(gw), False, k == 15 and f == 16)
-        for i in range(3):
-            firsts2(i + 3, ("B3", "B5", "B7")[i], rr[i])
-        for b in range(8):
-            mm(R("B2", 8 * b, 8 * b + 8), R("IND", 128 * b, 128 * b + 128), R("GS0"), True, True)
-        tc(R("OCB"), R("B2", 0, 64))
-        mm(R("B2", 128, 192), R("TRJ"), R("OCB"), True, False)
-        for j in range(1, 8):
-            mm(R("B2", 128 + 8 * j, 192), R("ONEB"), R("OCB", 0, 64 - 8 * j), False, j == 7)
-        for h in range(2):
-            for j in range(8):
-                mm(R("B2", 192 + 8 * h, 200 + 8 * h), R("ONEB"), R("OCB", 8 * j, 8 * j + 8), j == 0, j == 7)
-        ts(S(NV), R("B2", 192, 208), -1.0, A.mult, 1024.0, A.add)
-        u, y = R("SM", 512, 576), R("SM", 576, 640)
-        tt(u, R("CI"), R("B2", 128, 192), A.subtract)
-        tt(y, R("B2", 128, 192), u, A.subtract)
-        ts(y, y, 1024.0, A.add)
-        tt(y, y, R("OCB"), A.mult)
-        tt(R("E1", 0, 1024, 16), y, u, A.add)
-        scan(R("B3", 0, 512), R("RM", 0, 512), R("E1", 0, 512), A.mult, A.add)
-        scan(R("B5", 0, 512), R("RM", 0, 512), R("E1", 512, 1024), A.mult, A.add)
-        tt(R("EM", 0, 512), R("B3"), R("QM", 0, 512), A.mult)
-        tt(R("EM", 512, 1024), R("B5"), R("QM", 0, 512), A.mult)
-        for b in range(8):
-            mm(R("B2", 256 + 8 * b, 264 + 8 * b), R("EM", 128 * b, 128 * b + 128), R("RB"), True, True)
-        tc(R("LST", 64, 128), R("B2", 256, 320))
-        tc(I("TB", 0, NE, "LST", 64, 128), R("TB", NE, NE + 1024))
-        scan(R("UD"), R("RM"), R("TD"), A.mult, A.max)
+        rr = [firsts(i, ("B3", "B7")[i]) for i in range(2)]
+        scan(R("KB"), R("RM", 0, 256), R("B0", 0, 256), A.mult, A.max)
+        tc(R("SI", 48, 64), R("KB", 15, 256, 16))
+        ts(R("SI", 48, 64), R("SI", 48, 64), 15, A.bitwise_and)
+        tt(R("E1", 0, 256, 16), C(1), R("SI", 48, 64), A.subtract)
+        w = wrap(16, "B2", "B1")
+        tc(R("LST", 16, 32), w)
+        tc(R("XB"), I("TX", 0, 4096, "LST", 16, 32))
+        xb = R("XB")
+        for i in range(2):
+            firsts2(rr[i])
+            rr.append(firsts(i + 2, ("B3", "B7")[i]))
+        for i in range(2):
+            firsts2(rr[i + 2])
+            rr.append(firsts(i + 4, ("B3", "B7")[i]))
         for h in range(2):
             for k in range(16):
                 mm(R("B0", 128 * h + k, 128 * h + 128, 16), R("TD", 2048 * h + k, 2048 * h + 2048, 16), g8, True, True)
-            mm(R("B1", 8 * h, 8 * h + 8), R("INDD", 128 * h, 128 * h + 128), g8, True, True)
+            mm(R("B1", 8 * h, 8 * h + 8), R("INDD", 128 * h, 128 * h + 128), g8, True, False)
+            mm(R("B1", 8 * h, 8 * h + 8), own(h, "IND"), g8, False, True)
         act(R("KA"), R("B0", 0, 256), F.Abs)
+
+        for i in range(2):
+            firsts2(rr[i + 4])
+        for h in range(2):
+            scan(half("UD", h), half("RM", h), half("TD", h), A.mult, A.max)
         tt(R("VM"), R("US", 15, 4096, 16), R("UD", 15, 4096, 16), A.max)
+        for kk in range(2):
+            squares("SQB", "TX", xb, ("B4", "B5")[kk], kk)
         for h in range(2):
             mm(R("B1", 16 + 8 * h, 24 + 8 * h), R("VM", 128 * h, 128 * h + 128), g8, True, True)
+        for kk in range(2, 8):
+            squares("SQB", "TX", xb, ("B4", "B5")[kk % 2], kk)
         scan(R("MSD"), R("BM"), R("KA"), A.max, A.min)
-        tt(S(FM), S(FM), C(2), A.is_equal)
-        tt(S(FM), S(FM), S(HAS), A.mult)
-        tt(S(T1), R("B1", 0, 16), S(NN), A.add)
-        ts(S(T1), S(T1), 16.0, A.is_le)
-        tt(S(FM), S(FM), S(T1), A.mult)
-        tt(S(MS), R("SI", 32, 48), R("MSD", 15, 256, 16), A.min)
-        tt(S(T2), R("B1", 16, 32), S(MS), A.subtract)
-        tt(S(T2), S(T2), R("LIM", 32, 48), A.is_le)
-        mer = R("SB", 0, 16)
-        tt(mer, S(FM), S(T2), A.mult)
         tt(S(GR), S(SUU), R("SI", 32, 48), A.subtract)
         tt(S(GR), S(GR), R("LIM", 16, 32), A.is_gt)
+        tt(S(FM), S(FM), C(2), A.is_equal)
+        tt(S(MS), R("SI", 32, 48), R("MSD", 15, 256, 16), A.min)
+        tt(S(FM), S(FM), S(HAS), A.mult)
+        tt(S(MS), S(MS), R("LIM", 32, 48), A.add)
+        ts(S(T1), R("B1", 0, 16), 16.0, A.is_le)
+        tt(S(T2), R("B1", 16, 32), S(MS), A.is_le)
+        tt(S(FM), S(FM), S(T1), A.mult)
+        mer = R("SB", 0, 16)
+        tt(mer, S(FM), S(T2), A.mult)
         ts(S(NM), mer, -1.0, A.mult, 1.0, A.add)
         tt(S(NM), S(NM), S(LIVE), A.mult)
         want = R("SB", 16, 32)
@@ -590,98 +592,103 @@ def rank_program(g, core, T, topo):
         ranks("B1", 16)
         mm(R("B1", 32, 48), R("ONEB"), mer, True, True)
         ts(S(T1), S(DD), float(NE), A.add)
-        tt(S(T1), S(T1), C(3), A.subtract)
-        tt(S(T1), S(T1), mer, A.mult)
         tt(S(T2), S(DD), C(6 + t), A.subtract)
+        tt(S(T1), S(T1), C(3), A.subtract)
         tt(S(T2), S(T2), mer, A.mult)
+        tt(S(T1), S(T1), mer, A.mult)
         tt(R("E1", 512, 768, 16), S(T2), C(6 + t), A.add)
         tc(S(RK), R("B1", 0, 16))
         tt(S(SPL), S(RK), S(NV), A.is_lt)
         tt(S(SPL), S(SPL), want, A.mult)
         tt(R("SB", 32, 48), S(NM), S(SPL), A.subtract)
         ranks("B0", 32)
+        for h in range(2):
+            leave(h, "SQB", (g8, R("GM1")), True)
         tt(S(T2), S(RK), C(3), A.subtract)
+        tt(S(RV), S(RK), C(10 + t), A.subtract)
         tt(S(T2), S(T2), S(SPL), A.mult)
+        tt(S(RV), S(RV), S(SPL), A.mult)
         tt(S(T1), S(T1), S(T2), A.add)
+        tt(R("E1", 256, 512, 16), S(RV), C(10 + t), A.add)
         tt(R("E1", 0, 256, 16), S(T1), C(3), A.add)
-        tt(S(T2), S(RK), C(10 + t), A.subtract)
-        tt(S(T2), S(T2), S(SPL), A.mult)
-        tt(R("E1", 256, 512, 16), S(T2), C(10 + t), A.add)
         ts(S(VIS), R("B0", 0, 16), 64.0, A.is_lt)
-        tt(S(VIS), S(VIS), R("SB", 32, 48), A.mult)
         tt(S(T2), R("B0", 0, 16), C(4), A.subtract)
+        tt(S(VIS), S(VIS), R("SB", 32, 48), A.mult)
         tt(S(T2), S(T2), S(VIS), A.mult)
         tt(R("E1", 768, 1024, 16), S(T2), C(4), A.add)
-        scan(R("B3"), R("RM", 0, 512), R("E1", 0, 512), A.mult, A.add)
-        scan(R("B5"), R("RM", 0, 512), R("E1", 512, 1024), A.mult, A.add)
-        tt(R("EM", 512, 1024), R("B5"), R("QM", 0, 512), A.mult)
-        tt(R("EM", 0, 512), R("B3"), R("QM", 0, 512), A.mult)
-        for b in (6, 7, 4, 5, 0, 1, 2, 3):
-            mm(R("B2", 8 * b, 8 * b + 8), R("EM", 128 * b, 128 * b + 128), R("RB"), True, True)
-        tc(R("LST", 128, 192), R("B2", 0, 64))
+        tc(R("LST", 128, 192), wide("B2", 0, (6, 7, 4, 5, 0, 1, 2, 3)))
         dst = (rank + 1 + t % (n - 1)) % n
         src = (rank - 1 - t % (n - 1)) % n
         tc(I("VS", 0, 336, "LST", 176, 192), xs)
-        send(dst, "XV%d" % t, 64, "VS", "va%d" % t, "vl%d" % t)
+        send(dst, "XV%d" % t, "VS", "va%d" % t, "vl%d" % t)
         tc(R("MD"), I("ML", 0, 1280, "LST", 160, 176))
         for h in range(2):
             o = R("B7", 256 * h, 256 * h + 256)
-            mm(o, own(h), (T.IXA[:, :, :], [("IXA", 0, 256, 1)]), True, False)
-            mm(o, R("MD", 128 * h, 128 * h + 128), (T.IXB[:, :, :], [("IXB", 0, 256, 1)]), False, True)
-        ts(R("E2", 0, 512, 32), S(SPL), -1.0, A.add, BIG, A.mult)
+            mm(o, own(h), R3("IXA", 0, 8, 0, 32), True, False)
+            mm(o, R("MD", 128 * h, 128 * h + 128), R3("IXB", 0, 8, 0, 32), False, True)
         ts(S(T1), mer, -2.0, A.mult, 1.0, A.add)
+        ts(R("E2", 0, 512, 32), S(SPL), -1.0, A.add, BIG, A.mult)
         tt(S(T1), S(T1), S(SPL), A.subtract)
-        ts(R("E2", 16, 512, 32), S(T1), BIG, A.mult)
-        scan(R("TH"), R("RM", 0, 512), R("E2"), A.mult, A.add)
-        tt(R("PRS"), R("B6"), R("TH"), A.is_ge)
-        ts(R("TH"), R("PRS"), -1.0, A.mult, 1.0, A.add)
         ts(S(AA), S(NN), -1.0, A.mult, 16.0, A.add)
+        ts(R("E2", 16, 512, 32), S(T1), BIG, A.mult)
         tt(S(AA), S(AA), mer, A.mult)
-        tt(R("TH", 16, 512, 32), R("TH", 16, 512, 32), S(AA), A.add)
-        scan(R("B3"), R("RM", 0, 512), R("TH"), A.mult, A.add)
-        ts(R("ZI"), R("B3"), 4369.0, A.mult)
+        scan(R("THB"), R("RM", 0, 512), R("E2"), A.mult, A.add)
+        tt(R("PRS"), R("B6"), R("THB"), A.is_ge)
+        ts(R("THC"), R("PRS"), -1.0, A.mult, 1.0, A.add)
+        tt(R("THC", 16, 512, 32), R("THC", 16, 512, 32), S(AA), A.add)
+        scan(R("THB"), R("RM", 0, 512), R("THC"), A.mult, A.add)
+        ts(R("ZI"), R("THB"), 4369.0, A.mult)
         ts(R("ZI"), R("ZI"), 4680, A.bitwise_and)
-        tt(R("B5"), R("ZI"), R("B7"), A.add)
-        tt(w2(), R("B5"), R("PRS"), A.mult)
-        tc((T.F2[:, :, :], [("F2", 0, 256, 1)]), R3("W", 0, 16, 16, 32))
+        tt(R("B3"), R("ZI"), R("B7"), A.add)
+        tt(w2(), R("B3"), R("PRS"), A.mult)
+        tc(R3("F2", 0, 16, 0, 16), R3("W", 0, 16, 16, 32))
         for h in range(2):
             mm(R("B0", 128 * h, 128 * h + 128), R3("F2", 8 * h, 8 * h + 8, 0, 16), R("IDK"), True, True)
-        tc(R("NWE", 0, 4096, 16), I("TB", 0, NE + 1280, "LST", 144, 160))
+        tc(R("XE", 0, 4096, 16), I("TB", 0, NE + 1280, "LST", 144, 160))
         tc(R("TG"), I("TB", 0, NE + 1280, "LST", 128, 144))
         for q in range(16):
             mm(R("B4", 0, 16), R("WQ", 128 * q, 128 * q + 128), R("TG", q, 256, 16), q == 0, q == 15)
+        if t < 3:
+            addup(R("SM", 400, 401), R("B1", 32, 48))
         tc(R("SI", 0, 256), R("B0", 0, 256))
         ts(R("SI", 0, 256), R("SI", 0, 256), 8191, A.bitwise_and)
         moved(R("SI", 0, 256), "MVO")
-        scan(R("VAL"), R("RM"), R("NWE"), A.mult, A.add)
-        act(I("OW", 0, NO, "MVO", 0, 256), R("VAL"), F.Silu)
+        settle("MVO")
         tc(R("LST", 48, 64), R("B4", 0, 16))
         for th, s in ((4096.0, 1), (512.0, 2), (64.0, 4)):
-            ts(R("B3"), w2(), -th, A.add, 0.0, A.max)
             ts(R("B5"), w2(), -th, A.mult, th * th, A.add)
+            ts(R("B3"), w2(), -th, A.add, 0.0, A.max)
             tt(R("TH"), w2(), R("B5"), A.min)
             ts(R3("W", 15, 16, 24, 32), R("TH", 504, 512), 0.0, A.max)
-            tt((T.W[:, 0:15, :], [("W", 0, 480, 1)]), R("TH", 0, 480), R("B3", s, 480 + s), A.max)
+            tt(R3("W", 0, 15, 0, 32), R("TH", 0, 480), R("B3", s, 480 + s), A.max)
             tt(R3("W", 15, 16, 0, 32 - s), R("TH", 480, 512 - s), R("B3", 480 + s, 512), A.max)
         h3 = lambda a, b: R3("H3", 0, 16, a, b)
-        ts(h3(0, 32), w2(), -8.0, A.add, 0.0, A.max)
         ts(R("B5"), w2(), -8.0, A.mult, 64.0, A.add)
+        ts(h3(0, 32), w2(), -8.0, A.add, 0.0, A.max)
         tt(w2(), w2(), R("B5"), A.min)
-        tt(R3("F1", 0, 16, 0, 16), R3("W", 0, 16, 0, 16), h3(8, 24), A.max)
         tt(R3("F2", 0, 16, 0, 8), R3("W", 0, 16, 16, 24), h3(24, 32), A.max)
         ts(R3("F2", 0, 16, 8, 16), R3("W", 0, 16, 24, 32), 0.0, A.max)
-        for j, f in ((0, "F1"), (256, "F2")):
+        tt(R3("F1", 0, 16, 0, 16), R3("W", 0, 16, 0, 16), h3(8, 24), A.max)
+        for j, f in ((256, "F2"), (0, "F1")):
             for h in range(2):
                 mm(R("B7", j + 128 * h, j + 128 * h + 128), R3(f, 8 * h, 8 * h + 8, 0, 16), R("IDK"), True, True)
-        tc(R("ML", cl, 1024, 4), R("B7", 0, 256))
         tc(R("L2"), R("B7", 256, 512))
+        tc(R("ML", cl, 1024, 4), R("B7", 0, 256))
         tc(I("ML", 0, 1280, "LST", 48, 64), R("L2"))
         if t < 3:
-            op("v", lambda: g.vector.tensor_reduce(T.SM[:, 400:401], T.B1[:, 32:48], AX, A.add), R("SM", 400, 401), [R("B1", 32, 48)])
+            act(R("IND"), ml, F.Sign)
             tc(R("SI", 240, 241), R("SM", 400, 401))
             ts(R("SI", 240, 241), R("SI", 240, 241), 15, A.bitwise_and)
             tc(R("SM", 400, 401), R("SI", 240, 241))
             ts(R("LIM", 32, 48), R("LIM", 0, 16), R("SM", 400, 401), A.add)
+        else:
+            ts(R("E1"), ml, 0.0, A.is_equal, 4097.0, A.mult)
+            tt(R("E1"), R("E1"), ml, A.add)
+            ts(R("E1"), R("E1"), -1.0, A.add)
+            dma("oy", T.ym[:, :], T.E1[:, :], R("E1")[1], [])
+            ms(R("KB"), 0.0)
+        ev = R("E1", 0, 128, 16, 0, 64) if t < 3 else R("KB", 0, 128, 16, 0, 64)
+        ew = R("E1", 0, 128, 1, 0, 64) if t < 3 else R("KB", 0, 128, 1, 0, 64)
         xv = "XV%d" % t
         arrive("va%d" % t, xv)
         for q in range(16):
@@ -689,9 +696,9 @@ def rank_program(g, core, T, topo):
         tc(R("SI", 0, 4), R("B2", 64, 68))
         ts(R("SI", 0, 4), R("SI", 0, 4), 4095, A.bitwise_and)
         ts(R("LST", 192, 196), R("SI", 0, 4), 1, A.add)
-        tc(R("OVG"), I("OW", 0, NO, "LST", 192, 196))
         tc(R("XVS", 0, 1024, 16), R(xv))
         scan(R("XVE"), R("RM", 0, 1024), R("XVS"), A.mult, A.add)
+        tc(R("OVG"), I("OW", 0, NO, "LST", 192, 196))
         for q in range(16):
             mm(R("B2", 64, 68), R("WQ", 128 * q, 128 * q + 128), R("OVG", q, 64, 16), q == 0, q == 15)
         tc(R("LST", 200, 204), R("B2", 64, 68))
@@ -701,29 +708,26 @@ def rank_program(g, core, T, topo):
         mm(R("B0", 0, 128, 1, 0, 64), R("ONEB", 0, 64, 1, 0, 1), row(128, 128), True, False)
         for k in range(16):
             mm(R("B0", k, 128, 16, 0, 64), R("SQV", k, 1024, 16), R("G16"), False, k == 15)
-        scan(R("KB", 0, 128, 1, 0, 64), R("BM", 0, 128, 1, 0, 64), R("B0", 0, 128, 1, 0, 64), A.max, A.min)
-        tc(R("SI", 0, 8, 1, 0, 64), R("KB", 15, 128, 16, 0, 64))
+        scan(R("KD", 0, 128, 1, 0, 64), R("BM", 0, 128, 1, 0, 64), R("B0", 0, 128, 1, 0, 64), A.max, A.min)
+        tc(R("SI", 0, 8, 1, 0, 64), R("KD", 15, 128, 16, 0, 64))
         ts(R("SI", 0, 8, 1, 0, 64), R("SI", 0, 8, 1, 0, 64), 15, A.bitwise_and)
-        tt(R("E1", 0, 128, 16, 0, 64), R("SI", 0, 8, 1, 0, 64), R("CO", 80, 88, 1, 0, 64), A.add)
-        scan(R("B3", 0, 128, 1, 0, 64), R("RM", 0, 128, 1, 0, 64), R("E1", 0, 128, 1, 0, 64), A.mult, A.add)
+        tt(ev, R("SI", 0, 8, 1, 0, 64), R("CO", 80, 88, 1, 0, 64), A.add)
+        scan(R("B3", 0, 128, 1, 0, 64), R("RM", 0, 128, 1, 0, 64), ew, A.mult, A.add)
         tt(R("EM", 0, 128, 1, 0, 64), R("B3", 0, 128, 1, 0, 64), R("QM", 0, 128, 1, 0, 64), A.mult)
         mm(R("B2", 64, 68), R("EM", 0, 128, 1, 0, 64), R("RB", 0, 4, 1, 0, 64), True, True)
         tc(R("LST", 208, 212), R("B2", 64, 68))
         tc(R("SI", 64, 128), I("VD", 0, 1024, "LST", 208, 212))
         ts(R("SI", 64, 128), R("SI", 64, 128), 1, A.arith_shift_right)
         tc(R("RET"), R("SI", 64, 128))
-        send(src, "ME%d" % t, 64, "RET", "ra%d" % t, "rl%d" % t)
+        send(src, "ME%d" % t, "RET", "ra%d" % t, "rl%d" % t)
+        if t < 3:
+            tc(R("OFO"), R("ML", cl + 1, 1024, 4))
+            empties()
         arrive("ra%d" % t, "ME%d" % t)
         tt(R("NX1"), I("ME%d" % t, 0, 336, "LST", 176, 192), xs, A.add)
         tc(I("X", 0, NX, "LST", 0, 16), R("NX1"))
-    dma("y", "ox", T.yx[:, :], T.X[:, 1:4097], R("X", 1, 4097)[1], [])
-    ts(R("VAL", 0, 1024), R("ML", 0, 1024), 0.0, A.is_equal, 4097.0, A.mult)
-    tt(R("VAL", 0, 1024), R("VAL", 0, 1024), R("ML", 0, 1024), A.add)
-    ts(R("VAL", 0, 1024), R("VAL", 0, 1024), -1.0, A.add)
-    dma("y", "oy", T.ym[:, :], T.VAL[:, 0:1024], R("VAL", 0, 1024)[1], [])
-    for k in ("dm", "dx", "da", "dl", "dw", "ox", "oy"):
-        g.sync.wait_ge(T.sem[k], count[k])
-    for k in ("v", "s", "p", "gg"):
+    dma("ox", T.yx[:, :], T.X[:, 1:4097], R("X", 1, 4097)[1], [])
+    for k in ("dm", "dx", "da", "dl", "dw", "ox", "oy", "v", "s", "p", "gg"):
         g.sync.wait_ge(T.sem[k], count[k])
     for t in range(4):
         for k in ("vl", "rl"):

from concourse.mybir import AluOpType as A, ActivationFunctionType as F, AxisListType
AX = AxisListType.X

NX = 4368
NO = 8576
NE = 2064
D0 = 4352
BIG = float(2 ** 20)


def _sb(spec):
    d = {}
    for dtype, names in spec.items():
        for x in names.split():
            k, w = x.split(":")
            d[k] = ("sbuf", [128] + [int(v) for v in w.split("x")], dtype)
    return d


SCRATCH = _sb({
    "bfloat16": "X:4368 TB:3344 TX:4096 US:4096 XE:4096 SQO:4096 SQ:4096 XA:4096 OWG:4096 RM:4096 ONEB:128 IDB:128 NID:128 "
                "IDV:128 BO:128 G16:8 G64:8 GM1:8 GS0:8 GC:64 BM:256 ROW:1792 WQ:2048 WT:2048 TRI:128 TRJ:128 RW1:512 RW2:512 "
                "IND:1024 XS:256 SB:64 OCB:64 CF:768 XB:256 VM:256 TG:256 PRS:512 E2:512 THB:512 "
                "VS:336 XVE:1024 XVS:1024 VD:1024 OVG:64 RET:64",
    "float32": "OW:8576 ML:1280 VAL:4096 ONE:128 IDF:128 IDK:128 GS0F:8 QM:1024 RB:8 IXA:8x32 IXB:8x32 DUM:256 CO:256 CI:64 "
               "LMF:8 LIM:64 K1:256 KM:256 KB:256 KD:256 E1:1024 EM:1024 EX:256 EQ:256 DS:256 SM:1024 TH:512 MD:256 W:16x32 "
               "H3:16x32 F1:16x16 F2:16x16",
    "int32": "AC:4368 MI:1024 QI:1280 LMI:2 WTI:1 SI:256",
    "uint16": "OFO:256 ACO:256 OFD:256 MVO:256 LST:512 HL:64"})
for _t in range(4):
    SCRATCH["XV%d" % _t] = ("sbuf", [128, 64], "bfloat16")
    SCRATCH["ME%d" % _t] = ("sbuf", [128, 336], "bfloat16")
for _b in range(8):
    SCRATCH["B%d" % _b] = ("psum", [128, 512], "float32")
SHARE = {"SQB": "SQ", "XSE": "SQ", "THC": "CF", "NX1": "VM", "INDD": "TG", "TD": "XA", "UD": "OWG", "FS": "TH", "KA": "K1", "MSD": "KM", "L2": "MD", "ZI": "QI", "SQV": "XVE"}
WIDTH = {k: v[1][1] for k, v in SCRATCH.items()}
WIDTH.update({"SQB": 4096, "XSE": 4096, "THC": 512, "NX1": 256, "INDD": 256, "TD": 4096, "UD": 4096, "FS": 512, "KA": 256, "MSD": 256, "L2": 256, "ZI": 512, "SQV": 1024})
SEMAPHORES = ["v", "s", "p", "gg", "dx", "da", "dm", "dl", "dw", "oy", "ox"] + ["%s%d" % (a, b) for a in ("va", "vl", "ra", "rl") for b in range(4)]
PSUM = ["B%d" % b for b in range(8)]
SIZE = {"float32": 4, "int32": 4, "bfloat16": 2, "uint16": 2}


def rank_program(g, core, T, topo):
    rank = T.rank_of(core)
    if rank is None:
        return
    n = len(T.cores)
    queue = {"v": g.vector, "s": g.scalar, "p": g.tensor, "gg": g, "y": g.sync}
    count = {}
    known = {q: {} for q in queue}
    clock = {}
    log = {}

    def R(b, lo=0, hi=None, st=1, p0=0, p1=128):
        hi = WIDTH[b] if hi is None else min(hi, WIDTH[b])
        b = SHARE.get(b, b)
        full = p0 == 0 and p1 == 128
        ap = T[b][:, lo:hi:st] if full else T[b][p0:p1, lo:hi:st]
        return (ap, [(b, lo, hi, st)])

    def R3(b, a0, a1, k0, k1):
        s = SCRATCH[b][1][2]
        return (T[b][:, a0:a1, k0:k1], [(b, a0 * s, a1 * s, 1)])

    def I(b, lo, hi, ob, o0, o1):
        b, ob = SHARE.get(b, b), SHARE.get(ob, ob)
        return (T[b][:, lo:hi].indirect(T[ob][:, o0:o1]), [(b, lo, hi, 1), (ob, o0, o1, 1)])

    def need(q, reads, writes, dma=False):
        out = []
        for regs, w in ((reads, False), (writes, True)):
            for (b, lo, hi, st) in regs:
                ps = b in PSUM
                if dma and w:
                    al = 16 // SIZE[SCRATCH[b][2]]
                    lo, hi, st = lo // al * al, -(-hi // al) * al, 1
                for (l2, h2, s2, w2, e, c, d2) in log.get(b, []):
                    if ps:
                        if e == q and (q == "p" or not (w or w2) or lo >= h2 or l2 >= hi):
                            continue
                    else:
                        if not (w or w2):
                            continue
                        if d2 and w2 and w:
                            al = 16 // SIZE[SCRATCH[b][2]]
                            l2, h2, s2 = l2 // al * al, -(-h2 // al) * al, 1
                        if lo >= h2 or l2 >= hi or (st == s2 and st > 1 and (lo - l2) % st):
                            continue
                    out.append((e, c))
        best = {}
        for e, c in out:
            best[e] = max(best.get(e, 0), c)
        for e, c in sorted(best.items(), key=lambda x: -x[1]):
            if known[q].get(e, 0) < c:
                queue[q].wait_ge(T.sem[e], c)
                for k, v in clock[(e, c)].items():
                    known[q][k] = max(known[q].get(k, 0), v)

    def done(q, e, inc, reads, writes, dma=False):
        count[e] = count.get(e, 0) + inc
        c = count[e]
        ck = dict(known[q])
        ck[e] = c
        clock[(e, c)] = ck
        for (b, lo, hi, st) in writes:
            keep = [r for r in log.get(b, []) if not (b not in PSUM and st == 1 and lo <= r[0] and r[1] <= hi)]
            log[b] = keep + [(lo, hi, st, True, e, c, dma)]
        for (b, lo, hi, st) in reads:
            l = log.setdefault(b, [])
            l[:] = [r for r in l if not (r[:4] == (lo, hi, st, False) and r[4] == e)]
            l.append((lo, hi, st, False, e, c, dma))
        for b in set(x[0] for x in reads + writes if x[0] in PSUM):
            if len(log[b]) > 60:
                m = {}
                for r in log[b]:
                    k = (r[4], r[3])
                    o = m.get(k)
                    m[k] = r if o is None else (min(o[0], r[0]), max(o[1], r[1]), 1, r[3], r[4], max(o[5], r[5]), r[6])
                log[b] = list(m.values())

    def op(q, f, out, ins):
        rd = [x for i in ins if isinstance(i, tuple) for x in i[1]]
        wr = list(out[1])
        if len(wr) > 1:
            rd = rd + wr[1:]
            wr = wr[:1]
        need(q, rd, wr)
        f().then_inc(T.sem[q], 1)
        done(q, q, 1, rd, wr)

    def ap(x):
        return x[0] if isinstance(x, tuple) else x

    def tc(o, i):
        op("v", lambda: g.vector.tensor_copy(o[0], i[0]), o, [i])

    def tt(o, a, b, f):
        op("v", lambda: g.vector.tensor_tensor(o[0], a[0], b[0], f), o, [a, b])

    def ts(o, a, s1, f1, s2=None, f2=None):
        if f2 is None:
            op("v", lambda: g.vector.tensor_scalar(o[0], a[0], ap(s1), None, f1), o, [a, s1])
        else:
            op("v", lambda: g.vector.tensor_scalar(o[0], a[0], ap(s1), ap(s2), f1, f2), o, [a, s1, s2])

    def ms(o, c):
        op("v", lambda: g.vector.memset(o[0], c), o, [])

    def scan(o, d0, d1, f0, f1):
        op("v", lambda: g.vector.tensor_tensor_scan(o[0], d0[0], d1[0], 0.0, f0, f1), o, [d0, d1])

    def addup(o, i):
        op("v", lambda: g.vector.tensor_reduce(o[0], i[0], AX, A.add), o, [i])

    def act(o, i, f):
        op("s", lambda: g.scalar.activation(o[0], i[0], f), o, [i])

    def mm(o, l, r, a, z):
        op("p", lambda: g.tensor.matmul(o[0], l[0], r[0], a, z), o, [l, r])

    def aff(o, i, pat, cmp, fill, base, cm):
        op("gg", lambda: g.affine_select(o[0], i[0], pat, cmp, fill, base, cm), o, [i])

    def iota(o, pat, base, cm):
        fl = SCRATCH[o[1][0][0]][2] != "int32"
        op("gg", lambda: g.iota(o[0], pat, base, cm, allow_small_or_imprecise_dtypes=fl), o, [])

    def dma(sem, o_ap, i_ap, reads, writes):
        need("y", reads, writes, True)
        g.sync.dma_start(o_ap, i_ap).then_inc(T.sem[sem], 16)
        done("y", sem, 16, reads, writes, True)

    def send(dst, ob, ib, rs, ls):
        eng = topo.engines(core, T.cores[dst])[:4]
        mask = sum(1 << e for e in eng)
        rid, pid, _se = topo.addr(T.cores[dst])
        i = R(ib, 0, 64)
        need("gg", i[1], [])
        g.remote_dma(T[ob][:, 0:64], i[0], T.sem[rs], T.sem[ls], pid, rid, mask)
        done("gg", ls, len(eng), i[1], [])

    def arrive(sem, b):
        count[sem] = 4
        clock[(sem, 4)] = {sem: 4}
        log.setdefault(b, []).append((0, 64, 1, True, sem, 4, True))

    def bounded(o, pat, base, cm, width):
        aff(o, o, pat, A.is_ge, 0.0, base, cm)
        aff(o, o, [[-s, k] for s, k in pat], A.is_ge, 0.0, width - 1 - base, -cm)

    q_ = lambda k: R("QM", k, k + 1)
    C = lambda a: R("CO", 16 * a, 16 * a + 16)
    S = lambda a, w=16: R("SM", 16 * a, 16 * a + w)
    g8 = R("BO", 0, 128, 16)
    row = lambda a, w: R("ROW", a, a + w, 1, 0, 1)
    lone = R("ONEB", 0, 128, 1, 0, 1)
    one = R("ONE")
    w2 = lambda: (T.W[:, :, :], [("W", 0, 512, 1)])

    def wrap(cols, bank, ps, keep=None):
        w = 16 * cols
        x = keep if keep is not None else R(ps, 0, w)
        scan(x, R("RM", 0, w), R("E1", 0, w), A.mult, A.add)
        tt(R("EM", 0, w), x, R("QM", 0, w), A.mult)
        for h in range(cols // 8):
            mm(R(bank, 8 * h, 8 * h + 8), R("EM", 128 * h, 128 * h + 128), R("RB"), True, True)
        return R(bank, 0, cols)

    def wide(bank, lo, order):
        scan(R("B3"), R("RM", 0, 512), R("E1", 0, 512), A.mult, A.add)
        scan(R("B7"), R("RM", 0, 512), R("E1", 512, 1024), A.mult, A.add)
        tt(R("EM", 512, 1024), R("B7"), R("QM", 0, 512), A.mult)
        tt(R("EM", 0, 512), R("B3"), R("QM", 0, 512), A.mult)
        for b in order:
            mm(R(bank, lo + 8 * b, lo + 8 * b + 8), R("EM", 128 * b, 128 * b + 128), R("RB"), True, True)
        return R(bank, lo, lo + 64)

    def moved(ids, b):
        ts(R("B1", 0, 256), ids, 0.0, A.is_equal)
        tt(R("EQ"), R("B1", 0, 256), R("DUM"), A.mult)
        tt(R("EQ"), R("EQ"), ids, A.add)
        tc(R(b), R("EQ"))

    def owners(b):
        mv = ("MVO", "OFD")[b % 2]
        moved(R("ML", 256 * b, 256 * b + 256), mv)
        tc(R("XE", 0, 4096, 16), R("TB", NE + 256 * b, NE + 256 * b + 256))
        settle(mv)

    def settle(mv):
        for h in range(2):
            v = R("VAL", 2048 * h, 2048 * h + 2048)
            scan(v, R("RM", 0, 2048), R("XE", 2048 * h, 2048 * h + 2048), A.mult, A.add)
            act(I("OW", 0, NO, mv, 128 * h, 128 * h + 128), v, F.Silu)

    mi = R("MI")
    dma("dm", T.MI[:, :], T.ml[:, :], [], mi[1])
    ms(R("X", 0, 16), -16.0)
    ms(R("X", 4096, NX), 0.0)
    ms(R("AC", 0, 8), 0)
    ms(R("AC", 4096, NX), 0)
    dma("dx", T.X[:, 1:4097], T.x0[:, :], [], R("X", 1, 4097)[1])
    for j in range(4):
        dma("da", T.AC[:, 1 + 1024 * j:1025 + 1024 * j], T.ac[:, :], [], R("AC", 1 + 1024 * j, 1025 + 1024 * j)[1])
    log["AC"] = [r[:5] + (64,) + r[6:] if r[4] == "da" else r for r in log["AC"]]
    dma("dl", T.LMI[:], T.lims[:, :], [], R("LMI")[1])
    dma("dw", T.WTI[:], T.wt[:, :], [], R("WTI")[1])
    iota(R("QI", 0, 1024), [[0, 64], [-1, 16]], 1024, 1)
    iota(R("QI", 1024, 1280), [[1, 256]], 0, 0)
    iota(R("DUM"), [[16, 256]], D0, 1)
    ms(R("XE"), 0.0)
    ms(R("RM"), 1.0)
    ms(R("RM", 0, 4096, 16), 0.0)
    ms(R("OW", 0, 16), 128.0)
    ms(one, 1.0)
    ts(R("QI", 0, 1024), R("QI", 0, 1024), 15, A.bitwise_and)
    ts(R("QM"), R("QI", 0, 1024), 0, A.is_equal)
    ms(R("SM", 4, 6), 0.0)
    for u in range(4):
        ts(R("SM", 6, 7), q_(2 + u), float(u), A.mult)
        tt(R("SM", 4, 5), R("SM", 4, 5), R("SM", 6, 7), A.add)
        tt(R("SM", 5, 6), R("SM", 5, 6), q_(2 + u), A.add)
    ci, cj = R("QI", 1024, 1280), R("SI")
    ts(cj, ci, 7, A.logical_shift_right)
    ts(R("K1"), cj, q_(0), A.mult, 128.0, A.add)
    ts(cj, ci, 127, A.bitwise_and)
    ts(R("KM"), cj, q_(1), A.mult)
    tt(R("K1"), R("K1"), R("KM"), A.add)
    ts(cj, ci, 3, A.bitwise_and)
    ts(R("KM"), cj, R("SM", 4, 5), A.is_equal, R("SM", 5, 6), A.mult)
    tt(R("TB", NE, NE + 256), R("K1"), R("KM"), A.add)
    ml = R("ML", 0, 1024)
    ts(ml, mi, 4096, A.is_equal, -4097, A.mult)
    tt(ml, ml, mi, A.add)
    ts(ml, ml, 1, A.add)
    owners(0)
    for b in range(1, 5):
        ts(R("SM", 7, 8), q_(0), 2.0 * b, A.mult)
        ts(R("TB", NE + 256 * b, NE + 256 * b + 256), R("TB", NE, NE + 256), R("SM", 7, 8), A.add)
    ms(R("ML", 1024, 1280), 0.0)
    act(R("IND"), ml, F.Sign)
    aff(R("IDF"), one, [[-1, 128]], A.is_equal, 0.0, 0, 1)
    ms(R("TH"), 1.0)
    for o, w, p in ((0, 128, ([[-16, 8], [0, 16]], 0, 1, 16)), (128, 8, ([[-16, 8]], 0, 1, 16)), (256, 128, ([[1, 128]], -1, -1, 200)),
                    (384, 128, ([[1, 128]], 0, -1, 200))):
        bounded(R("TH", o, o + w), *p)
    tc(R("BO"), R("TH", 0, 128))
    tc(R("RB"), R("TH", 128, 136))
    tc(R("TRI"), R("TH", 256, 384))
    tc(R("TRJ"), R("TH", 384, 512))
    tc(R("ONEB"), one)
    tc(R("IDB"), R("IDF"))
    ts(R("NID"), R("IDF"), -1.0, A.mult)
    ts(R("IDK"), R("IDF"), 1024.0, A.mult)
    ts(R("IDV"), R("IDF"), float(2 ** 18), A.mult)
    for b, c in (("G16", 16.0), ("G64", 65536.0), ("GM1", -1.0)):
        ts(R(b), g8, c, A.mult)
    ts(R("GS0"), g8, q_(0), A.mult)
    ts(R("GS0F"), g8, q_(0), A.mult)
    for o, pat, base in ((0, [[0, 8], [4096, 16]], 0), (128, [[0, 8], [1, 16]], 0), (256, [[0, 8], [-1, 16]], 15), (512, [[-1, 256]], 0)):
        w = pat[0][1] * (pat[1][1] if len(pat) > 1 else 1)
        iota(R("EM", o, o + w), pat, base, 0)
    tc(R("ROW", 0, 384), R("EM", 0, 384))
    ms(R("ROW", 384, 512), -1.0)
    tc(R("ROW", 512, 768), R("EM", 512, 768))
    ms(w2(), 0.0)
    ms(R3("W", 0, 16, 16, 32), -1.0)
    tc(R("ROW", 768, 1280), w2())
    ms(R("ROW", 1280, 1792), 0.0)
    for h in range(2):
        tc(R("ROW", 1280 + 256 * h, 1408 + 256 * h), R("EM", 128, 256))
    ms(R("BM"), 0.0)
    ms(R("BM", 0, 256, 16), float(2 ** 25))
    wc = R("SM", 0, 1)
    ts(wc, q_(0), 128.0, A.mult)
    tt(wc, wc, q_(1), A.add)
    ts(R("SM", 1, 2), q_(6), -129.0, A.mult)
    tt(wc, wc, R("SM", 1, 2), A.add)
    for u in range(4):
        tt(R("SM", 2, 3), q_(2 + u), q_(6), A.subtract)
        ts(R("GC", 16 * u + 8, 16 * u + 16), g8, wc, A.mult)
        ts(R("GC", 16 * u, 16 * u + 8), g8, R("SM", 2, 3), A.mult, float(2 ** 17), A.mult)
    lanes = lambda a, base, s: iota(C(a), [[128 * s, 2], [0, 8]], base, s)
    lanes(0, 4097, 1)
    lanes(1, 15, 16)
    lanes(2, 4096, -1)
    lanes(3, NE + 1024, 1)
    lanes(4, 64, 1)
    iota(C(5), [[0, 16]], 0, 16)
    for t in range(4):
        lanes(6 + t, t, 4)
        lanes(10 + t, t + NE, 4)
    iota(R("CI"), [[128, 8], [0, 8]], 0, 1)
    iota(R("SI", 0, 1), [[0, 1]], 0, 1)
    ms(R("E1"), 0.0)
    ms(R("WQ"), 1.0)
    aff(R("WQ"), R("WQ"), [[1, 16], [0, 8], [-1, 16]], A.is_equal, 0.0, 0, 0)
    bounded(R("WQ"), [[0, 16], [-16, 8], [0, 16]], 0, 1, 16)
    owners(1)

    def rest():
        ms(R("TB", 0, NE), 128.0)
        for b, s in (("RW1", 128), ("RW2", 256)):
            ms(R(b), 1.0)
            ms(R(b, 0, 512, s), 0.0)
        ms(R3("IXA", 0, 8, 16, 32), 0.0)
        ms(R3("IXB", 0, 8, 0, 16), 0.0)
        ts(R3("IXA", 0, 8, 0, 16), R("IDF"), 2.0 ** -10, A.mult)
        ts(R3("IXB", 0, 8, 16, 32), R("IDF"), 2.0 ** -10, A.mult)
        for k in range(11):
            ms(R("SM", 16 + k, 17 + k), float(2 ** (10 - k)))
        ms(R("SM", 27, 32), 0.0)
        tt(R("SM", 16, 32), R("SM", 16, 32), R("QM", 0, 16), A.mult)
        addup(R("LMF", 0, 1), R("SM", 16, 32))
        ts(R("LMF", 2, 3), R("LMF", 1, 2), -1.0, A.mult, 1.0, A.add)
        for a in (0, 1):
            ts(R("LMF", 3 + 2 * a, 4 + 2 * a), R("LMF", 1 + a, 2 + a), 1 / 32, A.mult)
            ts(R("LMF", 4 + 2 * a, 5 + 2 * a), R("LMF", 1 + a, 2 + a), -16.0, A.mult)
        tc(R("SM", 8, 10), R("LMI"))
        for j in range(2):
            ts(R("VM", 0, 128), one, R("SM", 8 + j, 9 + j), A.mult)
            for h in range(2):
                mm(R("B2", 16 * j + 8 * h, 16 * j + 8 * h + 8), R("VM", 0, 128), R("GS0"), True, True)
        tc(R("LIM", 0, 32), R("B2", 0, 32))
        tc(R("LIM", 32, 48), R("LIM", 0, 16))
        for b in ("VS", "XVS", "E2"):
            ms(R(b), 0.0)
        for u in range(4):
            ms(R("ME%d" % u, 64, 336), 0.0)
        tc(R("SM", 3, 4), R("WTI"))
        ts(R("WT"), R("WQ"), R("SM", 3, 4), A.mult)
        ts(R("WQ"), R("WQ"), wc, A.mult)

    ts(R("SI", 0, 1), R("SI", 0, 1), 16, A.bitwise_and)
    ts(R("LMF", 1, 2), R("SI", 0, 1), 16.0, A.is_equal)
    NN, LIVE, HAS, FM, DD, MS, GR, WAN, SPL, RK, IDL, VIS, T1, T2, RV = range(4, 19)
    SUU, S1, NV, NM, AA = 20, 21, 22, 23, 24

    def empties():
        for b in range(8):
            mm(R("B2", 64 + 8 * b, 72 + 8 * b), R("IND", 128 * b, 128 * b + 128), R("GS0"), True, True)
        tc(R("OCB"), R("B2", 64, 128))
        mm(R("B2", 128, 192), R("TRJ"), R("OCB"), True, False)
        for j in range(1, 8):
            mm(R("B2", 128 + 8 * j, 192), R("ONEB"), R("OCB", 0, 64 - 8 * j), False, j == 7)
        for h in range(2):
            for j in range(8):
                mm(R("B2", 192 + 8 * h, 200 + 8 * h), R("ONEB"), R("OCB", 8 * j, 8 * j + 8), j == 0, j == 7)
        u, y = R("SM", 512, 576), R("SM", 576, 640)
        tt(u, R("CI"), R("B2", 128, 192), A.subtract)
        ts(S(NV), R("B2", 192, 208), -1.0, A.mult, 1024.0, A.add)
        tt(y, R("B2", 128, 192), u, A.subtract)
        ts(y, y, 1024.0, A.add)
        tt(y, y, R("OCB"), A.mult)
        tt(R("E1", 0, 1024, 16), y, u, A.add)
        tc(R("LST", 64, 128), wide("B2", 256, range(8)))
        tc(I("TB", 0, NE, "LST", 64, 128), R("TB", NE, NE + 1024))

    for t in range(4):
        cl = t & 3
        own = lambda h, b="ML": R(b, cl + 512 * h, cl + 512 * h + 512, 4)
        half = lambda b, h: R(b, 2048 * h, 2048 * h + 2048)

        def squares(out, win, w, bank, kk):
            for j in range(2):
                o = R(bank, 256 * j, 256 * j + 256)
                mm(o, R("IDB"), R(win, 2 * kk + j, 4096, 16), True, False)
                mm(o, R("NID"), w, False, True)
            act(R(out, 512 * kk, 512 * kk + 512), R(bank), F.Square)
        if t == 0:
            tc(R("OFO"), R("ML", 0, 1024, 4))
        tc(half("TX", 0), I("X", 0, NX, "OFO", 0, 128))
        if t == 0:
            tc(half("TX", 1), I("X", 0, NX, "OFO", 128, 256))
        else:
            act(half("TX", 1), I("X", 0, NX, "OFO", 128, 256), F.Copy)
        for h in range(2):
            o = R("B0", 128 * h, 128 * h + 128)
            mm(o, own(h), R("IDF"), True, False)
            mm(o, lone, row(0, 128), False, False)
            mm(o, lone, row(384, 128), False, False)
            for k in range(16):
                mm(R("B0", 128 * h + k, 128 * h + 128, 16), R("TX", 2048 * h + k, 2048 * h + 2048, 16), R("G64"), False, k == 15)
        act(R("K1"), R("B0", 0, 256), F.Abs)
        for h in range(2):
            mm(R("B2", 8 * h, 8 * h + 8), own(h, "IND"), g8, True, True)
        scan(half("US", 0), half("RM", 0), half("TX", 0), A.mult, A.max)
        tc(S(NN), R("B2", 0, 16))
        ts(S(LIVE), S(NN), 0.0, A.is_gt)
        scan(R("KM"), R("BM"), R("K1"), A.max, A.min)
        tc(R("SI", 0, 16), R("KM", 15, 256, 16))
        ts(R("SI", 16, 32), R("SI", 0, 16), 4095, A.bitwise_and)
        ts(S(T1), R("SI", 16, 32), 1.0, A.add)
        tt(S(T1), S(T1), C(0), A.subtract)
        tt(S(T1), S(T1), S(LIVE), A.mult)
        tt(R("E1", 0, 256, 16), S(T1), C(0), A.add)
        w = wrap(16, "B2", "B3")
        tc(R("LST", 0, 16), w)
        ts(R("ACO"), I("AC", 0, NX, "LST", 0, 16), 1, A.add)
        xs = R("XS")
        tc(xs, I("X", 0, NX, "LST", 0, 16))
        if t == 0:
            owners(2)
        tc(R("XE", 0, 4096, 16), xs)
        scan(R("XSE"), R("RM"), R("XE"), A.mult, A.add)
        if t == 0:
            owners(3)
        for h in range(2):
            act(half("OWG", h), I("OW", 0, NO, "ACO", 128 * h, 128 * h + 128), F.Copy)
        for h in range(2):
            tt(half("XA", h), I("X", 0, NX, "ACO", 128 * h, 128 * h + 128), half("XSE", h), A.subtract)
            act(half("XA", h), half("XA", h), F.Square)
        if t == 0:
            rest()
            empties()
        ts(R("SI", 32, 48), R("SI", 0, 16), 16, A.logical_shift_right)
        scan(half("US", 1), half("RM", 1), half("TX", 1), A.mult, A.max)
        for h in range(2):
            mm(R("B2", 16 + 8 * h, 24 + 8 * h), R("US", 2048 * h + 15, 2048 * h + 2048, 16), g8, True, True)
        tc(S(SUU), R("B2", 16, 32))
        mm(R("B0"), lone, row(1280, 512), True, False)
        for h in range(2):
            for k in range(16):
                mm(R("B0", 256 * h + k, 256 * h + 256, 16), R("OWG", 2048 * h + k, 2048 * h + 2048, 16), R("GC", 16 * cl, 16 * cl + 16), False, False)
        for h in range(2):
            for k in range(16):
                mm(R("B0", 256 * h + k, 256 * h + 128, 16), R("XA", 2048 * h + k, 2048 * h + 2048, 16), R("G16"), False, h == 1 and k == 15)
        for kk in range(5):
            squares("SQO", "TX", xs, ("B4", "B5")[kk % 2], kk)
        hv = lambda b, h: R(b, 128 * h, 128 * h + 128)
        for h in range(2):
            scan(hv("KD", h), R("BM", 0, 128), R("B0", 256 * h, 256 * h + 128), A.max, A.min)
        tc(R("E1", 0, 256, 16), R("KD", 15, 256, 16))
        scan(R("EX"), R("RM", 0, 256), R("E1", 0, 256), A.mult, A.add)
        for h in range(2):
            tt(hv("EQ", h), hv("EX", h), R("B0", 256 * h, 256 * h + 128), A.is_equal)
        for h in range(2):
            tt(hv("EQ", h), hv("EQ", h), R("B0", 256 * h + 128, 256 * h + 256), A.mult)
        scan(R("DS"), R("RM", 0, 256), R("EQ"), A.mult, A.add)
        ts(S(HAS), R("KD", 15, 256, 16), float(2 ** 17), A.is_lt)
        tt(S(HAS), S(HAS), S(LIVE), A.mult)
        ts(S(T1), R("DS", 15, 256, 16), float(-cl), A.add)
        tt(S(T1), S(T1), S(HAS), A.mult)
        ts(S(DD), S(T1), float(cl), A.add)
        tc(R("E1", 0, 256, 16), S(DD))
        w = wrap(16, "B2", "B3", R("EX"))
        for h in range(2):
            mm(R("B1", 128 * h, 128 * h + 128), R("EX", 128 * h, 128 * h + 128), R("IDF"), True, True)
        for kk in range(5, 8):
            squares("SQO", "TX", xs, ("B4", "B5")[kk % 2], kk)
        tc(R("LST", 32, 48), w)
        tc(R("MD"), I("ML", 0, 1280, "LST", 32, 48))
        tc(R("OFD"), R("MD"))
        for h in range(2):
            act(half("TD", h), I("X", 0, NX, "OFD", 128 * h, 128 * h + 128), F.Copy)
        act(R("INDD"), R("MD"), F.Sign)
        ts(R("ZI", 0, 256), R("B1", 0, 256), R("LMF", 0, 1), A.mult)
        ts(R("ZI", 0, 256), R("ZI", 0, 256), 1024, A.bitwise_and)
        ts(R("CF", 0, 256), R("ZI", 0, 256), 1 / 32, A.mult, -16.0, A.add)
        ts(R("CF", 256, 512), R("ZI", 0, 256), R("LMF", 5, 6), A.mult, R("LMF", 6, 7), A.add)
        ts(R("CF", 512, 768), R("ZI", 0, 256), R("LMF", 3, 4), A.mult, R("LMF", 4, 5), A.add)
        for h in range(2):
            o = R("B0", 128 * h, 128 * h + 128)
            mm(o, own(h, "IND"), R("IDV"), True, False)
            mm(o, lone, row(256, 128), False, False)
            for k in range(16):
                mm(R("B0", 128 * h + k, 128 * h + 128, 16), R("SQO", 256 * k + 128 * h, 256 * k + 128 * h + 128), R("G16"), False, k == 15)

        def leave(h, sq, signs, stop):
            for k in range(16):
                for f in range(2):
                    mm(R("B6", 256 * h + 16 * f + k, 256 * h + 256, 32), R(sq, 256 * k + 128 * h, 256 * k + 128 * h + 128), signs[f], False,
                       stop and h == 1 and k == 15 and f == 1)
        mm(R("B6"), lone, row(768, 512), True, False)
        for h in range(2):
            leave(h, "SQO", (R("GM1"), g8), False)

        def firsts(i, b):
            if i < 2:
                h, gs, wd, rw = 0, range(4 * i, 4 * i + 4), 128, "RW1"
            else:
                h, gs, wd, rw = 1, range(2 * (i - 2), 2 * (i - 2) + 2), 256, "RW2"
            for j, gg in enumerate(gs):
                p0 = 32 * (gg // 2)
                o = R(b, wd * j, wd * j + wd)
                if j and p0 != 32 * (gs[j - 1] // 2):
                    queue["p"].wait_ge(T.sem["p"], count["p"])
                    known["p"]["p"] = count["p"]
                mm(o, R("ONEB", 0, 128, 1, p0, p0 + 1), R("ROW", 512, 512 + wd, 1, p0, p0 + 1), True, False)
                c = 256 + 256 * (gg % 2) + 128 * h
                mm(o, R("CF", c, c + 128, 1, p0, p0 + 32), R("CF", 0, wd, 1, p0, p0 + 32), False, True)
            return gs, wd, rw, h, b

        def firsts2(r):
            gs, wd, rw, h, b = r
            scan(R("FS"), R(rw), R(b), A.mult, A.max)
            tc(R("SM", 16 * FM + 8 * h + gs[0], 16 * FM + 8 * h + gs[0] + len(gs)), R("FS", wd - 1, 512, wd))
        rr = [firsts(i, ("B3", "B7")[i]) for i in range(2)]
        scan(R("KB"), R("RM", 0, 256), R("B0", 0, 256), A.mult, A.max)
        tc(R("SI", 48, 64), R("KB", 15, 256, 16))
        ts(R("SI", 48, 64), R("SI", 48, 64), 15, A.bitwise_and)
        tt(R("E1", 0, 256, 16), C(1), R("SI", 48, 64), A.subtract)
        w = wrap(16, "B2", "B1")
        tc(R("LST", 16, 32), w)
        tc(R("XB"), I("TX", 0, 4096, "LST", 16, 32))
        xb = R("XB")
        for i in range(2):
            firsts2(rr[i])
            rr.append(firsts(i + 2, ("B3", "B7")[i]))
        for i in range(2):
            firsts2(rr[i + 2])
            rr.append(firsts(i + 4, ("B3", "B7")[i]))
        for h in range(2):
            for k in range(16):
                mm(R("B0", 128 * h + k, 128 * h + 128, 16), R("TD", 2048 * h + k, 2048 * h + 2048, 16), g8, True, True)
            mm(R("B1", 8 * h, 8 * h + 8), R("INDD", 128 * h, 128 * h + 128), g8, True, False)
            mm(R("B1", 8 * h, 8 * h + 8), own(h, "IND"), g8, False, True)
        act(R("KA"), R("B0", 0, 256), F.Abs)

        for i in range(2):
            firsts2(rr[i + 4])
        for h in range(2):
            scan(half("UD", h), half("RM", h), half("TD", h), A.mult, A.max)
        tt(R("VM"), R("US", 15, 4096, 16), R("UD", 15, 4096, 16), A.max)
        for kk in range(2):
            squares("SQB", "TX", xb, ("B4", "B5")[kk], kk)
        for h in range(2):
            mm(R("B1", 16 + 8 * h, 24 + 8 * h), R("VM", 128 * h, 128 * h + 128), g8, True, True)
        for kk in range(2, 8):
            squares("SQB", "TX", xb, ("B4", "B5")[kk % 2], kk)
        scan(R("MSD"), R("BM"), R("KA"), A.max, A.min)
        tt(S(GR), S(SUU), R("SI", 32, 48), A.subtract)
        tt(S(GR), S(GR), R("LIM", 16, 32), A.is_gt)
        tt(S(FM), S(FM), C(2), A.is_equal)
        tt(S(MS), R("SI", 32, 48), R("MSD", 15, 256, 16), A.min)
        tt(S(FM), S(FM), S(HAS), A.mult)
        tt(S(MS), S(MS), R("LIM", 32, 48), A.add)
        ts(S(T1), R("B1", 0, 16), 16.0, A.is_le)
        tt(S(T2), R("B1", 16, 32), S(MS), A.is_le)
        tt(S(FM), S(FM), S(T1), A.mult)
        mer = R("SB", 0, 16)
        tt(mer, S(FM), S(T2), A.mult)
        ts(S(NM), mer, -1.0, A.mult, 1.0, A.add)
        tt(S(NM), S(NM), S(LIVE), A.mult)
        want = R("SB", 16, 32)
        tt(want, S(GR), S(NM), A.mult)

        def ranks(bank, s):
            mm(R(bank, 0, 8), R("TRI"), R("SB", s, s + 8), True, True)
            mm(R(bank, 8, 16), R("TRI"), R("SB", s + 8, s + 16), True, False)
            mm(R(bank, 8, 16), R("ONEB"), R("SB", s, s + 8), False, True)
        ranks("B1", 16)
        mm(R("B1", 32, 48), R("ONEB"), mer, True, True)
        ts(S(T1), S(DD), float(NE), A.add)
        tt(S(T2), S(DD), C(6 + t), A.subtract)
        tt(S(T1), S(T1), C(3), A.subtract)
        tt(S(T2), S(T2), mer, A.mult)
        tt(S(T1), S(T1), mer, A.mult)
        tt(R("E1", 512, 768, 16), S(T2), C(6 + t), A.add)
        tc(S(RK), R("B1", 0, 16))
        tt(S(SPL), S(RK), S(NV), A.is_lt)
        tt(S(SPL), S(SPL), want, A.mult)
        tt(R("SB", 32, 48), S(NM), S(SPL), A.subtract)
        ranks("B0", 32)
        for h in range(2):
            leave(h, "SQB", (g8, R("GM1")), True)
        tt(S(T2), S(RK), C(3), A.subtract)
        tt(S(RV), S(RK), C(10 + t), A.subtract)
        tt(S(T2), S(T2), S(SPL), A.mult)
        tt(S(RV), S(RV), S(SPL), A.mult)
        tt(S(T1), S(T1), S(T2), A.add)
        tt(R("E1", 256, 512, 16), S(RV), C(10 + t), A.add)
        tt(R("E1", 0, 256, 16), S(T1), C(3), A.add)
        ts(S(VIS), R("B0", 0, 16), 64.0, A.is_lt)
        tt(S(T2), R("B0", 0, 16), C(4), A.subtract)
        tt(S(VIS), S(VIS), R("SB", 32, 48), A.mult)
        tt(S(T2), S(T2), S(VIS), A.mult)
        tt(R("E1", 768, 1024, 16), S(T2), C(4), A.add)
        tc(R("LST", 128, 192), wide("B2", 0, (6, 7, 4, 5, 0, 1, 2, 3)))
        dst = (rank + 1 + t % (n - 1)) % n
        src = (rank - 1 - t % (n - 1)) % n
        tc(I("VS", 0, 336, "LST", 176, 192), xs)
        send(dst, "XV%d" % t, "VS", "va%d" % t, "vl%d" % t)
        tc(R("MD"), I("ML", 0, 1280, "LST", 160, 176))
        for h in range(2):
            o = R("B7", 256 * h, 256 * h + 256)
            mm(o, own(h), R3("IXA", 0, 8, 0, 32), True, False)
            mm(o, R("MD", 128 * h, 128 * h + 128), R3("IXB", 0, 8, 0, 32), False, True)
        ts(S(T1), mer, -2.0, A.mult, 1.0, A.add)
        ts(R("E2", 0, 512, 32), S(SPL), -1.0, A.add, BIG, A.mult)
        tt(S(T1), S(T1), S(SPL), A.subtract)
        ts(S(AA), S(NN), -1.0, A.mult, 16.0, A.add)
        ts(R("E2", 16, 512, 32), S(T1), BIG, A.mult)
        tt(S(AA), S(AA), mer, A.mult)
        scan(R("THB"), R("RM", 0, 512), R("E2"), A.mult, A.add)
        tt(R("PRS"), R("B6"), R("THB"), A.is_ge)
        ts(R("THC"), R("PRS"), -1.0, A.mult, 1.0, A.add)
        tt(R("THC", 16, 512, 32), R("THC", 16, 512, 32), S(AA), A.add)
        scan(R("THB"), R("RM", 0, 512), R("THC"), A.mult, A.add)
        ts(R("ZI"), R("THB"), 4369.0, A.mult)
        ts(R("ZI"), R("ZI"), 4680, A.bitwise_and)
        tt(R("B3"), R("ZI"), R("B7"), A.add)
        tt(w2(), R("B3"), R("PRS"), A.mult)
        tc(R3("F2", 0, 16, 0, 16), R3("W", 0, 16, 16, 32))
        for h in range(2):
            mm(R("B0", 128 * h, 128 * h + 128), R3("F2", 8 * h, 8 * h + 8, 0, 16), R("IDK"), True, True)
        tc(R("XE", 0, 4096, 16), I("TB", 0, NE + 1280, "LST", 144, 160))
        tc(R("TG"), I("TB", 0, NE + 1280, "LST", 128, 144))
        for q in range(16):
            mm(R("B4", 0, 16), R("WQ", 128 * q, 128 * q + 128), R("TG", q, 256, 16), q == 0, q == 15)
        if t < 3:
            addup(R("SM", 400, 401), R("B1", 32, 48))
        tc(R("SI", 0, 256), R("B0", 0, 256))
        ts(R("SI", 0, 256), R("SI", 0, 256), 8191, A.bitwise_and)
        moved(R("SI", 0, 256), "MVO")
        settle("MVO")
        tc(R("LST", 48, 64), R("B4", 0, 16))
        for th, s in ((4096.0, 1), (512.0, 2), (64.0, 4)):
            ts(R("B5"), w2(), -th, A.mult, th * th, A.add)
            ts(R("B3"), w2(), -th, A.add, 0.0, A.max)
            tt(R("TH"), w2(), R("B5"), A.min)
            ts(R3("W", 15, 16, 24, 32), R("TH", 504, 512), 0.0, A.max)
            tt(R3("W", 0, 15, 0, 32), R("TH", 0, 480), R("B3", s, 480 + s), A.max)
            tt(R3("W", 15, 16, 0, 32 - s), R("TH", 480, 512 - s), R("B3", 480 + s, 512), A.max)
        h3 = lambda a, b: R3("H3", 0, 16, a, b)
        ts(R("B5"), w2(), -8.0, A.mult, 64.0, A.add)
        ts(h3(0, 32), w2(), -8.0, A.add, 0.0, A.max)
        tt(w2(), w2(), R("B5"), A.min)
        tt(R3("F2", 0, 16, 0, 8), R3("W", 0, 16, 16, 24), h3(24, 32), A.max)
        ts(R3("F2", 0, 16, 8, 16), R3("W", 0, 16, 24, 32), 0.0, A.max)
        tt(R3("F1", 0, 16, 0, 16), R3("W", 0, 16, 0, 16), h3(8, 24), A.max)
        for j, f in ((256, "F2"), (0, "F1")):
            for h in range(2):
                mm(R("B7", j + 128 * h, j + 128 * h + 128), R3(f, 8 * h, 8 * h + 8, 0, 16), R("IDK"), True, True)
        tc(R("L2"), R("B7", 256, 512))
        tc(R("ML", cl, 1024, 4), R("B7", 0, 256))
        tc(I("ML", 0, 1280, "LST", 48, 64), R("L2"))
        if t < 3:
            act(R("IND"), ml, F.Sign)
            tc(R("SI", 240, 241), R("SM", 400, 401))
            ts(R("SI", 240, 241), R("SI", 240, 241), 15, A.bitwise_and)
            tc(R("SM", 400, 401), R("SI", 240, 241))
            ts(R("LIM", 32, 48), R("LIM", 0, 16), R("SM", 400, 401), A.add)
        else:
            ts(R("E1"), ml, 0.0, A.is_equal, 4097.0, A.mult)
            tt(R("E1"), R("E1"), ml, A.add)
            ts(R("E1"), R("E1"), -1.0, A.add)
            dma("oy", T.ym[:, :], T.E1[:, :], R("E1")[1], [])
            ms(R("KB"), 0.0)
        ev = R("E1", 0, 128, 16, 0, 64) if t < 3 else R("KB", 0, 128, 16, 0, 64)
        ew = R("E1", 0, 128, 1, 0, 64) if t < 3 else R("KB", 0, 128, 1, 0, 64)
        xv = "XV%d" % t
        arrive("va%d" % t, xv)
        for q in range(16):
            mm(R("B2", 64, 68), R("WT", 128 * q, 128 * q + 128), R(xv, q, 64, 16), q == 0, q == 15)
        tc(R("SI", 0, 4), R("B2", 64, 68))
        ts(R("SI", 0, 4), R("SI", 0, 4), 4095, A.bitwise_and)
        ts(R("LST", 192, 196), R("SI", 0, 4), 1, A.add)
        tc(R("XVS", 0, 1024, 16), R(xv))
        scan(R("XVE"), R("RM", 0, 1024), R("XVS"), A.mult, A.add)
        tc(R("OVG"), I("OW", 0, NO, "LST", 192, 196))
        for q in range(16):
            mm(R("B2", 64, 68), R("WQ", 128 * q, 128 * q + 128), R("OVG", q, 64, 16), q == 0, q == 15)
        tc(R("LST", 200, 204), R("B2", 64, 68))
        tc(R("HL"), I("ML", 0, 1280, "LST", 200, 204))
        tt(R("VD"), I("X", 0, NX, "HL", 0, 64), R("XVE"), A.subtract)
        act(R("SQV"), R("VD"), F.Square)
        mm(R("B0", 0, 128, 1, 0, 64), R("ONEB", 0, 64, 1, 0, 1), row(128, 128), True, False)
        for k in range(16):
            mm(R("B0", k, 128, 16, 0, 64), R("SQV", k, 1024, 16), R("G16"), False, k == 15)
        scan(R("KD", 0, 128, 1, 0, 64), R("BM", 0, 128, 1, 0, 64), R("B0", 0, 128, 1, 0, 64), A.max, A.min)
        tc(R("SI", 0, 8, 1, 0, 64), R("KD", 15, 128, 16, 0, 64))
        ts(R("SI", 0, 8, 1, 0, 64), R("SI", 0, 8, 1, 0, 64), 15, A.bitwise_and)
        tt(ev, R("SI", 0, 8, 1, 0, 64), R("CO", 80, 88, 1, 0, 64), A.add)
        scan(R("B3", 0, 128, 1, 0, 64), R("RM", 0, 128, 1, 0, 64), ew, A.mult, A.add)
        tt(R("EM", 0, 128, 1, 0, 64), R("B3", 0, 128, 1, 0, 64), R("QM", 0, 128, 1, 0, 64), A.mult)
        mm(R("B2", 64, 68), R("EM", 0, 128, 1, 0, 64), R("RB", 0, 4, 1, 0, 64), True, True)
        tc(R("LST", 208, 212), R("B2", 64, 68))
        tc(R("SI", 64, 128), I("VD", 0, 1024, "LST", 208, 212))
        ts(R("SI", 64, 128), R("SI", 64, 128), 1, A.arith_shift_right)
        tc(R("RET"), R("SI", 64, 128))
        send(src, "ME%d" % t, "RET", "ra%d" % t, "rl%d" % t)
        if t < 3:
            tc(R("OFO"), R("ML", cl + 1, 1024, 4))
            empties()
        arrive("ra%d" % t, "ME%d" % t)
        tt(R("NX1"), I("ME%d" % t, 0, 336, "LST", 176, 192), xs, A.add)
        tc(I("X", 0, NX, "LST", 0, 16), R("NX1"))
    dma("ox", T.yx[:, :], T.X[:, 1:4097], R("X", 1, 4097)[1], [])
    for k in ("dm", "dx", "da", "dl", "dw", "ox", "oy", "v", "s", "p", "gg"):
        g.sync.wait_ge(T.sem[k], count[k])
    for t in range(4):
        for k in ("vl", "rl"):
            g.wait_ge(T.sem["%s%d" % (k, t)], count["%s%d" % (k, t)])
